import numpy as np, ml_dtypes
CORES = [23,119,17,113]
N = 4
BF = ml_dtypes.bfloat16
def gentries(a):
    return np.ascontiguousarray(a.reshape(8, 16, -1).transpose(0, 2, 1)).reshape(8, -1)
def gtable(e):
    e = np.asarray(e); return np.ascontiguousarray(e.reshape(8, -1, 16).transpose(0, 2, 1)).reshape(128, -1).astype(np.int32)
C, D, S, CAP, TH, HOP = 3072, 256, 4, 64, 12, 1
R = C // 16
def inverse(A):
    O = np.zeros_like(A); np.put_along_axis(O, A, np.broadcast_to(np.arange(C), A.shape), -1)
    return O
def estates(A, Y):
    V = np.zeros_like(Y)
    for k in range(16): V += np.take_along_axis(Y, A[:, :, k:k + 1, :], 3)
    return V
def judge(A, O, V, Y, h, z):
    n = h.shape[1]
    ca = np.take_along_axis(A, h[:, None, :], 2)
    yv = np.take_along_axis(Y, ca.reshape(8, 1, 16 * n), 2).reshape(8, 16, 16, n)
    k = np.argmax(np.add.reduce(np.minimum(yv, z[:, :, None, :]), axis=1), axis=1)
    a = np.take_along_axis(ca, k[:, None, :], 1)[:, 0]
    co = np.take_along_axis(O, a[:, None, :], 2)
    vv = np.take_along_axis(V, co.reshape(8, 1, 16 * n), 2).reshape(8, 16, 16, n)
    vc = np.take_along_axis(V, h[:, None, :], 2)
    over = np.add.reduce((vv > vc[:, :, None, :]).astype(np.int64), axis=1)
    j = np.argmax(over, axis=1)[:, None, :]
    return k, a, np.take_along_axis(co, j, 1)[:, 0], np.take_along_axis(over, j, 1)[:, 0]
def meets(x):
    eq = np.any(x[:, None, :, None] == x[None, :, None, :], axis=(2, 3))
    return np.any(np.tril(eq, -1), axis=1)
def exchange(A, O, V, Y, c, f, k, a):
    b = A[k, f]
    ok = ~(meets(np.stack([c, f], 1)) | meets(np.stack([a, b], 1)))
    c, f, k, a, b = c[ok], f[ok], k[ok], a[ok], b[ok]
    A[k, c] = b; A[k, f] = a; O[k, a] = f; O[k, b] = c
    dv = Y[:, b] - Y[:, a]
    V[:, c] += dv; V[:, f] -= dv
def cities(rng):
    rc = np.argsort(rng.random((N, 8, C)), axis=-1); ra = np.argsort(rng.random((N, 8, C)), axis=-1)
    key = rng.random((N, 8, 16, C)); key[:, :, 1:, :R] -= 1.0
    A = np.take_along_axis(ra[:, :, None, :], np.argsort(key, axis=-1), 3)
    A = np.take_along_axis(A, np.argsort(rc, axis=-1)[:, :, None, :], 3)
    m = np.zeros((N, 8, C), bool); np.put_along_axis(m, ra[:, :, :R], True, -1)
    Y = rng.integers(0, 16, (N, 8, 16, C)); Y = np.where(m[:, :, None, :], (Y >> 1) + 8, Y)
    return A, Y, np.ascontiguousarray(rc[:, :, :R])
def duties(rng, rc, n):
    h = np.where(rng.random((N, 8, n)) < 0.125, np.take_along_axis(rc, rng.integers(0, R, (N, 8, n)), 2), rng.integers(0, C, (N, 8, n)))
    top = rng.choice(np.array([0, 1, 3, 7, 7, 11, 15, 15, 15, 15]), (N, 8, 1, n))
    return h, rng.integers(0, top + 1, (N, 8, 16, n))
def ring(rng, A, Y, g, T):
    pc = np.argsort(rng.random((N, C)), axis=-1); pa = np.argsort(rng.random((N, C)), axis=-1)
    for q in range(N):
        A[q, g][:, pc[q]] = pa[q][(np.arange(C)[None, :] + np.arange(16)[:, None]) % C]
        Y[q, g][:, pa[q]] = T[q][:, np.arange(C) % 16]
    return pc
def pack(A, Y, h, z):
    O = inverse(A); V = estates(A, Y)
    w = lambda x: np.ascontiguousarray(x.reshape(N, 128, -1)).astype(np.float32).astype(BF)
    return {"ao": np.ascontiguousarray((A + 4096 * O).reshape(N, 128, C)).astype(np.int32), "yd": w(Y), "ve": w(V), "hd": np.stack([gtable(x) for x in h]), "zc": w(z)}
def setup_inputs(rng):
    A, Y, rc = cities(rng); h, z = duties(rng, rc, D)
    return pack(A, Y, h, z)
def setup_inputs_room(rng):
    A, Y, rc = cities(rng); h4, z4 = duties(rng, rc, 4 * D); O = inverse(A); V = estates(A, Y)
    h = np.zeros((N, 8, D), np.int64); z = np.zeros((N, 8, 16, D), np.int64)
    for q in range(N):
        k, a, f, m = judge(A[q], O[q], V[q], Y[q], h4[q], z4[q]); prop = (m < TH) & (f != h4[q])
        for g in range(8):
            yes = np.nonzero(prop[g])[0]; no = np.nonzero(~prop[g])[0]; ver = np.nonzero(m[g] >= TH)[0]
            if len(yes) == 0: yes = no
            if len(no) == 0: no = yes
            n = int(rng.choice(np.array([0, 1, CAP - 1, CAP, CAP + 1, D])))
            if q == 0: n = (CAP, CAP + 1, D, CAP - 1, 1, 0, CAP, CAP + 1)[g]
            if n == 0 and q % 2 == 0 and len(ver) > 0: no = ver
            ix = rng.permutation(np.concatenate([np.resize(rng.permutation(yes), n), np.resize(rng.permutation(no), D - n)]))
            h[q, g] = h4[q, g, ix]; z[q, g] = z4[q, g][:, ix]
    return pack(A, Y, h, z)
def setup_inputs_clash(rng):
    A, Y, rc = cities(rng); h, z = duties(rng, rc, D); iq = np.arange(N)
    T = rng.integers(0, 11, (N, 16, 16)); w = rng.integers(0, 16, N); T[iq, :, w] = 15
    p2 = ring(rng, A, Y, 2, T)
    T = rng.integers(0, 11, (N, 16, 16)); c4 = rng.integers(0, C, N); ks = np.argsort(rng.random((N, 15)), axis=-1)[:, :2] + 1
    T[iq, :8, (c4 + ks[:, 0]) % 16] = 15; T[iq, 8:, (c4 + ks[:, 1]) % 16] = 15
    p4 = ring(rng, A, Y, 4, T)
    e = int(rng.integers(0, C)); s = int(rng.integers(0, C)); r16 = np.arange(16)
    for q in range(N):
        at = np.argmax(A[q, 6] == s, axis=1); A[q, 6][r16, at] = A[q, 6][r16, e]; A[q, 6][r16, e] = s
    O = inverse(A)
    few = rng.integers(0, C, (N, 8, 24)); hf = np.take_along_axis(few, rng.integers(0, 24, (N, 8, D)), 2)
    st = np.argsort(rng.random((N, 8, C)), axis=-1)[:, :, None, :12]
    own = np.take_along_axis(O, st, 3).reshape(N, 8, 192); ho = np.take_along_axis(own, rng.integers(0, 192, (N, 8, D)), 2)
    Y2 = Y.copy(); np.put_along_axis(Y2, np.broadcast_to(st, (N, 8, 16, 12)), 15, 3)
    Y[:, 1::2] = Y2[:, 1::2]; h[:, ::2] = hf[:, ::2]; h[:, 1::2] = ho[:, 1::2]
    z[:, 1::2] = rng.integers(8, 16, (N, 4, 16, D))
    gap = C // CAP // 16 * 16
    for q in range(N):
        d = rng.permutation(D)[:CAP]; k = rng.integers(1, 16, CAP)
        z[q, 2] = 0; z[q, 2][:, d] = 15; h[q, 2, d] = p2[q, gap * np.arange(CAP) + (w[q] - k) % 16]
    kind = (np.arange(D)[None, :] + rng.integers(0, 2, (N, 1))) % 2
    h[:, 4] = p4[iq, c4][:, None]; z[:, 4] = np.where((np.arange(16) < 8)[None, :, None] == (kind == 0)[:, None, :], 15, 0)
    h[int(rng.integers(0, N)), 6] = e
    return pack(A, Y, h, z)
def setup_inputs_ties(rng):
    A, Y, rc = cities(rng); h, z = duties(rng, rc, D)
    lo = rng.integers(0, 4, (N, 8, 1, 1)); hi = lo + rng.integers(1, 12, (N, 8, 1, 1))
    Y = np.where(rng.random((N, 8, 16, C)) < 0.5, lo, hi)
    z = np.where(rng.random((N, 8, 1, D)) < 0.5, rng.integers(0, 16, (N, 8, 1, D)), z)
    g = rng.permutation(8); Y[:, g[0]] = rng.integers(1, 16, (N, 1, 1)); z[:, g[1]] = 0
    Y[:, g[2]] = rng.integers(14, 16, (N, 16, C)); z[:, g[2]] = np.where(rng.random((N, 1, D)) < 0.5, 15, rng.integers(14, 16, (N, 16, D)))
    return pack(A, Y, h, z)
def setup_inputs_ends(rng):
    A, Y, rc = cities(rng); h, z = duties(rng, rc, D)
    A[:, 1] = np.arange(C); A[:, 2] = (np.arange(C)[None, :] + np.arange(16)[:, None]) % C; A[:, 3] = A[:, 2]
    Y[..., 0] = 15; Y[..., C - 1] = 15; O = inverse(A)
    T = rng.integers(0, 16, (N, 16, 16)); Y[:, 3] = T[:, :, np.arange(C) % 16]
    own = np.ascontiguousarray(O[..., [0, C - 1]]).reshape(N, 8, 32)
    u = rng.random((N, 8, D)); e = rng.choice(np.array([0, C - 1]), (N, 8, D))
    h = np.where(u < 0.4, np.take_along_axis(own, rng.integers(0, 32, (N, 8, D)), 2), np.where(u < 0.5, e, h))
    h[..., 0] = 0; h[..., D - 1] = C - 1
    return pack(A, Y, h, z)
def setup_inputs_spread(rng):
    A, Y, rc = cities(rng); h, z = duties(rng, rc, D)
    s = np.exp2(4 * rng.random((N, 8, 1, C))) * np.exp2(-2 * rng.random((N, 8, 16, 1)))
    Y = np.minimum((s * rng.random((N, 8, 16, C))).astype(np.int64), 15)
    Y[rng.random(Y.shape) < 0.05] = 15
    z = np.minimum((np.exp2(5 * rng.random((N, 8, 1, D))) * rng.random((N, 8, 16, D))).astype(np.int64), 15)
    return pack(A, Y, h, z)
def check_inputs(d):
    bad = []
    for k, hi in (("yd", 15), ("zc", 15), ("ve", 240)):
        x = np.asarray(d[k]).astype(np.float32)
        if not np.all((x >= 0) & (x <= hi) & (x == np.floor(x))): bad.append("range of " + k)
    if np.min(d["hd"]) < 0 or np.max(d["hd"]) > C - 1: bad.append("range of hd")
    ao = np.asarray(d["ao"]).astype(np.int64).reshape(N, 8, 16, C); A = ao & 4095; O = ao >> 12
    if np.min(ao) < 0 or np.max(A) > C - 1 or np.max(O) > C - 1: return bad + ["range of ao"]
    m = np.zeros(A.shape, bool); np.put_along_axis(m, A, True, -1)
    if not np.all(m): bad.append("a row of A is no permutation")
    if not np.all(np.take_along_axis(O, A, 3) == np.arange(C)): bad.append("O is not the inverse of A")
    if not bad:
        Y = np.asarray(d["yd"]).astype(np.float32).astype(np.int64).reshape(N, 8, 16, C)
        if not np.all(estates(A, Y) == np.asarray(d["ve"]).astype(np.float32).astype(np.int64).reshape(N, 8, 16, C)): bad.append("ve is not the sum of the yields")
    return bad
def reference(ao, yd, ve, hd, zc):
    w = ao.astype(np.int64).reshape(N, 8, 16, C); A = w & 4095; O = w >> 12
    Y = yd.astype(np.float32).astype(np.int64).reshape(N, 8, 16, C); V = ve.astype(np.float32).astype(np.int64).reshape(N, 8, 16, C)
    z = zc.astype(np.float32).astype(np.int64).reshape(N, 8, 16, D); h = np.stack([gentries(x) for x in hd]).astype(np.int64)
    log = []
    for t in range(S):
        new = []
        for q in range(N):
            k, a, f, m = judge(A[q], O[q], V[q], Y[q], h[q], z[q])
            for g in range(8):
                ix = np.nonzero((m[g] < TH) & (f[g] != h[q, g]))[0][:CAP]
                exchange(A[q, g], O[q, g], V[q, g], Y[q, g], h[q, g, ix], f[g, ix], k[g, ix], a[g, ix])
            new.append(np.where(m >= TH, f, h[q]))
        h = np.stack(new); log.append(h)
        if t < S - 1:
            h = np.roll(h, HOP, axis=0); z = np.roll(z, HOP, axis=0)
    return {"vo": V.reshape(N, 128, C).astype(np.float32).astype(BF), "ho": np.stack(log, axis=2).reshape(N, 8, S * D).astype(np.float32)}

@@ -1,0 +1,487 @@
+import numpy as np
+from concourse.mybir import AluOpType as ALU, ActivationFunctionType as AF
+
+N, C, D, S, HOP = 4, 3072, 256, 4, 1
+PAD = 2 * C
+V1, V2 = 192, 160
+MAGIC = 1.5 * 2.0 ** 35
+F, B, H, I32, U16 = "float32", "bfloat16", "float16", "int32", "uint16"
+SCRATCH = {}
+for _n, _w, _d in (
+        ("aoraw", C, I32), ("AO", PAD + 256, I32), ("VY", PAD + 256, B), ("z0", D, B), ("zin", 3 * D, B),
+        ("z16a", 16 * D, B), ("z16b", 16 * D, B), ("mn", 16 * D, B), ("gy", 1536, B), ("vc", D, B), ("vcx", 16 * V2, B),
+        ("hdi", 16, I32), ("hdo", 16, F), ("hl0", 16, U16), ("hin", 96, U16), ("hsend", 96, U16),
+        ("ca", D, U16), ("cah", D, H), ("sc", D, F), ("rn", 16, F), ("af", 16, F), ("bi", 16, I32), ("ki", 16, I32),
+        ("TM", D, H), ("la", 16, U16), ("hT", 16, F), ("hn", 16, F), ("ver", 16, F), ("nz", 16, F), ("prop", 16, B), ("df", 16, F), ("rp", 16, F),
+        ("vz", 2304, H), ("oh", 1024, H), ("rs16", 64, H), ("rb16", 64, H), ("LM", D, F), ("LS", D, F), ("gl", 16, U16),
+        ("K64", 64, F), ("prod", 64, F), ("E", 1280, H), ("KD", D, F), ("NW", D, I32), ("vg", D, B), ("nv", 128, B),
+        ("PM", D, F), ("PS", D, F), ("of", 16, F), ("so", 16, U16), ("hob", 512, F),
+        ("ipi", 1, I32), ("ip", 1, F), ("p16i", 1, I32), ("pgi", 1, I32), ("p16", 1, F), ("pg", 1, F), ("kcode", 1, F), ("sv", 16, F),
+        ("i128", 128, F), ("imod", D, F), ("idiv", 128, F), ("ipad", D, F),
+        ("If", 128, F), ("Ih", 128, H), ("Ib", 128, B), ("Inb", 128, B), ("U", 128, B), ("on", 128, B), ("m256", D, F), ("bo", 128, F),
+        ("boh", 128, H), ("jjh", 8, H), ("blk", 8, B), ("nblk", 8, B), ("hblk", 8, B), ("zblk", 128, B), ("rst", D, F), ("brow", 128, B),
+        ("am", 128, B), ("c524", 128, B), ("io64", 64, H), ("exl", 16, U16), ("mk", 64, B), ("mkb", 64, B),
+        ("DP", D, F), ("k8192", 64, B), ("k3072", 64, B), ("hneg", 512, B),
+        ("se0", 128, H), ("se2", 128, H), ("se3", 128, H), ("se4n", 128, H), ("se0n", 128, H), ("se2n", 128, H),
+        ("sd", 128, H), ("sdn", 128, H), ("sb0", 128, H), ("sb1", 128, H), ("sb2", 128, H)):
+    SCRATCH[_n] = ("sbuf", [128, _w], _d)
+for _i in range(8):
+    SCRATCH["P%d" % _i] = ("psum", [128, 512], F)
+SEMAPHORES = ["cV", "cA", "cP", "cG"] + ["d%d" % i for i in range(24)] + ["az1", "az2", "az3", "ah1", "ah2", "ah3", "lz", "lh"]
+
+
+def rank_program(g, core, T, topo):
+    rank = T.rank_of(core)
+    if rank is None:
+        return
+    Q = {"V": g.vector, "A": g.scalar, "P": g.tensor, "G": g, "S": g.sync}
+    cnt = {}
+    seen = {q: {} for q in Q}
+    snap = {}
+    Wr, Rd = {}, {}
+    toks = [None]
+
+    def new_token(q, sem, n):
+        cnt[sem] = cnt.get(sem, 0) + n
+        toks.append((sem, cnt[sem], q))
+        snap[len(toks) - 1] = dict(seen[q])
+        return len(toks) - 1
+
+    def wait_tok(q, i):
+        sem, v, _ = toks[i]
+        if seen[q].get(sem, 0) >= v:
+            return
+        Q[q].wait_ge(T.sem[sem], v)
+        seen[q][sem] = v
+        for s2, v2 in snap[i].items():
+            if v2 > seen[q].get(s2, 0):
+                seen[q][s2] = v2
+
+    def track(name):
+        if name not in Wr:
+            Wr[name] = np.zeros(SCRATCH[name][1][1], np.int64)
+            Rd[name] = {}
+
+    def need(q, reads, writes):
+        ids = set()
+        for kind, accs in ((0, reads), (1, writes)):
+            for name, cols in accs:
+                track(name)
+                if SCRATCH[name][0] == "psum":
+                    for arr in list(Rd[name].values()) + [Wr[name]]:
+                        ids.update(int(x) for x in np.unique(arr) if x and toks[int(x)][2] != q)
+                else:
+                    ids.update(int(x) for x in np.unique(Wr[name][cols]))
+                    if kind:
+                        for arr in Rd[name].values():
+                            ids.update(int(x) for x in np.unique(arr[cols]))
+        ids.discard(0)
+        if q == "P":
+            ids = {i for i in ids if toks[i][0] != "cP"}
+        for i in sorted(ids, reverse=True):
+            wait_tok(q, i)
+
+    def note(tok, reads, writes):
+        key = toks[tok][0]
+        for name, cols in reads:
+            Rd[name].setdefault(key, np.zeros(len(Wr[name]), np.int64))[cols] = tok
+        for name, cols in writes:
+            Wr[name][cols] = tok
+
+    def op(q, call, writes, reads):
+        rr = [a for x in reads for a in x[1]]
+        ww = [a for x in writes for a in x[1]]
+        need(q, rr, ww)
+        call().then_inc(T.sem["c" + q], 1)
+        note(new_token(q, "c" + q, 1), rr, ww)
+
+    def X(name, a=None, b=None, s=1, p=None):
+        a = 0 if a is None else a
+        b = SCRATCH[name][1][1] if b is None else b
+        ps = slice(None) if p is None else slice(p[0], p[1])
+        ap = T[name][ps, a:b] if s == 1 else T[name][ps, a:b:s]
+        return (ap, [(name, np.arange(a, b, s))])
+
+    def IND(win, off):
+        return (win[0].indirect(off[0]), win[1] + off[1])
+
+    def cp(o, i):
+        op("V", lambda: g.vector.tensor_copy(o[0], i[0]), [o], [i])
+
+    def tt(o, a, b, f):
+        op("V", lambda: g.vector.tensor_tensor(o[0], a[0], b[0], f), [o], [a, b])
+
+    def ts(o, a, s1, f1, s2=None, f2=None):
+        rs = [a]
+        v1, v2 = s1, s2
+        if isinstance(s1, tuple):
+            rs.append(s1)
+            v1 = s1[0]
+        if isinstance(s2, tuple):
+            rs.append(s2)
+            v2 = s2[0]
+        if f2 is None:
+            op("V", lambda: g.vector.tensor_scalar(o[0], a[0], v1, None, f1), [o], rs)
+        else:
+            op("V", lambda: g.vector.tensor_scalar(o[0], a[0], v1, v2, f1, f2), [o], rs)
+
+    def scan(o, d0, d1, f1):
+        op("V", lambda: g.vector.tensor_tensor_scan(o[0], d0[0], d1[0], 0.0, ALU.mult, f1), [o], [d0, d1])
+
+    def act(o, i, f=AF.Copy, bias=0.0):
+        op("A", lambda: g.scalar.activation(o[0], i[0], f, bias=bias), [o], [i])
+
+    def mm(o, l, r, start, stop):
+        op("P", lambda: g.tensor.matmul(o[0], l[0], r[0], start, stop), [o], [l, r])
+
+    def iota(o, pat, base, cm):
+        if SCRATCH[o[1][0][0]][2] == I32:
+            op("G", lambda: g.iota(o[0], pat, base, cm), [o], [])
+        else:
+            op("G", lambda: g.iota(o[0], pat, base, cm, allow_small_or_imprecise_dtypes=True), [o], [])
+
+    nd = [0]
+
+    def dma(q, o, i):
+        need(q, i[1], o[1])
+        sem = "d%d" % nd[0]
+        nd[0] += 1
+        Q[q].dma_start(o[0], i[0]).then_inc(T.sem[sem], 16)
+        note(new_token(q, sem, 16), i[1], o[1])
+
+    def send(dst, name, a, b, name2, a2, rsem, lsem):
+        src = X(name, a, b)
+        need("G", src[1], [])
+        rid, pid, _ = topo.addr(dst)
+        eng = topo.engines(core, dst)[:8]
+        g.remote_dma(T[name2][:, a2:a2 + b - a], src[0], T.sem[rsem], T.sem[lsem], pid, rid, sum(1 << e for e in eng))
+        note(new_token("G", lsem, len(eng)), src[1], [])
+
+    def arrives(name, a, b, rsem, src):
+        track(name)
+        cnt[rsem] = len(topo.engines(src, core)[:8])
+        toks.append((rsem, cnt[rsem], "R"))
+        snap[len(toks) - 1] = {}
+        Wr[name][a:b] = len(toks) - 1
+
+    EQ, MU, AD, SU = ALU.is_equal, ALU.mult, ALU.add, ALU.subtract
+    dma("S", X("hdi"), (T.hd[:, :], []))
+    dma("A", X("z0"), (T.zc[:, :], []))
+    for i in range(4):
+        w = C // 4
+        dma("SA"[i % 2], X("aoraw", i * w, i * w + w), (T.ao[:, i * w:i * w + w], []))
+    dma("S", X("VY", C, C + C // 2), (T.yd[:, 0:C // 2], []))
+    dma("A", X("VY", C + C // 2, PAD), (T.yd[:, C // 2:C], []))
+    dma("S", X("VY", 0, C // 2), (T.ve[:, 0:C // 2], []))
+    dma("A", X("VY", C // 2, C), (T.ve[:, C // 2:C], []))
+    iota(X("ipi"), [[0, 1]], 0, 1)
+    iota(X("ip"), [[0, 1]], 0, 1)
+    iota(X("i128"), [[1, 128]], 0, 0)
+    iota(X("imod"), [[0, 16], [1, 16]], 0, 0)
+    iota(X("idiv"), [[1, 8], [0, 16]], 0, 0)
+    iota(X("on"), [[0, 128]], 1, 0)
+    iota(X("ipad"), [[1, 256]], PAD, 0)
+    iota(X("c524"), [[0, 128]], 524288, 0)
+    iota(X("mk", 16, 64), [[0, 48]], 0, 0)
+    iota(X("mkb", 16, 64), [[0, 48]], 4608, 0)
+    iota(X("k8192"), [[0, 64]], 8192, 0)
+    iota(X("k3072"), [[0, 64]], 3072, 0)
+    for r in range(1, N):
+        send(T.cores[(rank + r * HOP) % N], "z0", 0, D, "zin", (r - 1) * D, "az%d" % r, "lz")
+        arrives("zin", (r - 1) * D, r * D, "az%d" % r, T.cores[(rank - r * HOP) % N])
+        arrives("hin", (r - 1) * 32, r * 32, "ah%d" % r, T.cores[(rank - HOP) % N])
+    p, p16, pg = X("ip"), X("p16"), X("pg")
+    ts(X("p16i"), X("ipi"), 15, ALU.bitwise_and)
+    ts(X("pgi"), X("ipi"), 4, ALU.logical_shift_right)
+    op("V", lambda: g.vector.memset(T.hneg[:, :], -0.5), [X("hneg")], [])
+    cp(X("hl0"), X("hdi"))
+    ts(X("hdo"), X("hdi"), -1536.0, AD)
+    cp(X("p16"), X("p16i"))
+    cp(X("pg"), X("pgi"))
+    cp(X("exl"), X("i128", 0, 16))
+    ts(X("jjh"), X("i128", 0, 8), pg, EQ)
+    ts(X("m256"), X("imod"), p16, EQ)
+    ts(X("Ib"), X("i128"), p, EQ)
+    ts(X("Inb"), X("i128"), p, EQ, -1.0, MU)
+    ts(X("Ih"), X("i128"), p, EQ)
+    ts(X("blk"), X("i128", 0, 8), pg, EQ, 65536.0, MU)
+    ts(X("nblk"), X("i128", 0, 8), pg, EQ, -65536.0, MU)
+    ts(X("hblk"), X("i128", 0, 8), pg, EQ, 32768.0, MU)
+    ts(X("zblk"), X("idiv"), pg, EQ, 65536.0, MU)
+    ts(X("brow"), X("imod", 0, 128), -4096.0, MU, 61440.0, AD)
+    ts(X("rst"), X("imod"), 0.0, ALU.not_equal)
+
+    def consts2():
+        ts(X("am"), X("i128"), float(V2 - 128), ALU.is_ge)
+        ts(X("U"), X("i128"), p, ALU.is_ge)
+        ts(X("If"), X("i128"), p, EQ)
+        ts(X("bo"), X("idiv"), pg, EQ)
+        ts(X("boh"), X("idiv"), pg, EQ, 8192.0, MU)
+        ts(X("kcode"), p16, -1.0, MU, 15.0, AD)
+        ts(X("io64"), X("i128", 0, 64), 1.0, AD)
+        for v in range(5):
+            ts(X("sv", v, v + 1), p16, float(v), EQ)
+        for v, c in ((0, 1536.0), (1, 1536.0), (2, 4608.0)):
+            ts(X("sv", 5 + v, 6 + v), p16, 4.0, EQ, c, MU)
+            tt(X("sv", 8 + v, 9 + v), X("sv", v, v + 1), X("sv", 5 + v, 6 + v), AD)
+
+    def consts3():
+        bo = X("bo")
+        for nm, v in (("se0", 0), ("se2", 2), ("se3", 3), ("sb0", 8), ("sb1", 9), ("sb2", 10)):
+            ts(X(nm), bo, X("sv", v, v + 1), MU)
+        ts(X("se4n"), bo, X("sv", 4, 5), MU, -8192.0, MU)
+        ts(X("se0n"), X("se0"), -1.0, MU)
+        ts(X("se2n"), X("se2"), -1.0, MU)
+        tt(X("sd"), X("sb1"), X("sb0"), SU)
+        ts(X("sdn"), X("sd"), -1.0, MU)
+
+    def consts4():
+        ts(X("mk", 0, 16), X("imod", 0, 16), p16, ALU.is_le, 16384.0, MU)
+        ts(X("mkb", 0, 16), X("mk", 0, 16), 4608.0, AD)
+        tt(X("DP"), X("m256"), X("ipad"), MU)
+        ts(X("vz", 0, 256), X("imod"), 0.0, MU)
+        cp(X("vz", 256, 512), X("vz", 0, 256))
+        cp(X("vz", 512, 1024), X("vz", 0, 512))
+        cp(X("vz", 1024, 2048), X("vz", 0, 1024))
+        cp(X("vz", 2048, 2304), X("vz", 0, 256))
+        ts(X("vz", 4, 2165, 144), X("imod", 0, 16), 0.0, MU, 1.0, AD)
+    blocks = []
+    o = 0
+    for q in range(4):
+        blocks.append((o, 64 - 16 * q))
+        o += 2 * (64 - 16 * q)
+
+    def expand_z(t):
+        src = X("z0") if t == 0 else X("zin", (t - 1) * D, t * D)
+        for k in range(16):
+            act(X(("z16a", "z16b")[t % 2], k, 16 * D, 16), src)
+
+    expand_z(0)
+    for i in range(4):
+        w = C // 4
+        ts(X("AO", i * w, i * w + w), X("aoraw", i * w, i * w + w), 4095, ALU.bitwise_and)
+        ts(X("AO", C + i * w, C + i * w + w), X("aoraw", i * w, i * w + w), 12, ALU.logical_shift_right)
+        (consts2, consts3, consts4, lambda: None)[i]()
+
+    def conv_a(src):
+        tt(X("TM"), IND(src, X("exl")), X("m256"), MU)
+
+    lists = X("P2", 128, 144)
+
+    def conv_b():
+        for hf in range(2):
+            mm(X("P2", 128 + 8 * hf, 136 + 8 * hf), X("TM", 128 * hf, 128 * hf + 128), X("jjh"), True, True)
+
+    conv_a(X("hdo"))
+    conv_b()
+    cp(X("hT"), lists)
+
+    def embed():
+        for hf in range(2):
+            mm(X("P%d" % hf, 0, 128), X("cah", 128 * hf, 128 * hf + 128), X("Ih"), True, False)
+
+    def reduce(d0, d1, w):
+        hf, b = d0 // 128, d0 % 128
+        for k in range(16):
+            mm(X("P%d" % hf, k, 128, 16, (b, b + d1 - d0)), X("mn", 16 * d0 + k, 16 * d1, 16), X(w), False, False)
+
+    def close(hf):
+        mm(X("P%d" % hf, 0, 128), X("on", p=(0, 1)), X("brow", p=(0, 1)), False, True)
+
+    def best_of(hf):
+        scan(X("sc", 128 * hf, 128 * hf + 128), X("rst", 0, 128), X("P%d" % hf, 0, 128), ALU.max)
+
+    na1, na2 = (D - V1) // 32, (D - V2) // 32
+    best = X("sc", 15, 256, 16)
+    for t in range(S):
+        last = t == S - 1
+        hl = X("hl0") if t == 0 else X("hin", (t - 1) * 32, (t - 1) * 32 + 16)
+        zrow = X("z0", V1, D) if t == 0 else X("zin", (t - 1) * D + V1, t * D)
+        z16 = ("z16a", "z16b")[t % 2]
+        for i, d0 in enumerate(range(V1, D, 32)):
+            mm(X("P%d" % (3 + i)), X("Ib"), X(z16, 16 * d0, 16 * d0 + 512), True, False)
+        cp(X("ca"), IND(X("AO", 0, C), hl))
+        ts(X("cah"), X("ca"), -1536.0, AD)
+        embed()
+        mm(X("P1", 0, 128, 1, (64, 128)), zrow, X("zblk"), False, False)
+        for i in range(na2):
+            mm(X("P%d" % (5 + i)), X("Ib"), X("hneg"), True, False)
+
+        def vmin(a, b):
+            tt(X("mn", 16 * a, 16 * b), IND(X("VY", C, PAD), X("ca", a, b)), X(z16, 16 * a, 16 * b), ALU.min)
+
+        def sub_vc(i):
+            for j in range(16):
+                mm(X("P%d" % (5 + i), j, 512, 16), X("Inb"), X("vc", V2 + 32 * i, V2 + 32 * i + 32), False, False)
+        vmin(128, V1)
+        for i, d0 in enumerate(range(V1, D, 32)):
+            act(X("gy", 512 * i, 512 * i + 512), IND(X("VY", C, PAD), X("ca", d0, d0 + 32)))
+            mm(X("P%d" % (3 + i)), X("Inb"), X("gy", 512 * i, 512 * i + 512), False, True)
+        for i, d0 in enumerate(range(V1, D, 32)):
+            act(X("mn", 16 * d0, 16 * d0 + 512), X("P%d" % (3 + i)), AF.Relu)
+        act(X("vc"), IND(X("VY", 0, C), hl))
+        for j in range(16):
+            act(X("vcx", j, 16 * V2, 16), X("vc", 0, V2))
+        reduce(128, V1, "blk")
+        vmin(0, 64)
+        reduce(0, 64, "blk")
+        vmin(64, 96)
+        reduce(V1, D, "nblk")
+        close(1)
+        reduce(64, 96, "blk")
+        vmin(96, 128)
+        reduce(96, 128, "blk")
+        close(0)
+        sub_vc(0)
+        if t:
+            ts(X("hT"), X("hin", (t - 1) * 32 + 16, t * 32), -1536.0, AD)
+        cp(X("vz", 0, 2161, 144), X("hT"))
+        best_of(1)
+        best_of(0)
+        ts(X("rn"), best, MAGIC, AD, MAGIC, SU)
+        tt(X("af"), best, X("rn"), SU)
+        conv_a(X("af"))
+        conv_b()
+        for i in range(1, na2):
+            sub_vc(i)
+        ts(X("bi"), X("rn"), 1.0 / 4096, MU)
+        cp(X("vz", 2, 2163, 144), X("af"))
+        ts(X("ki"), X("bi"), 15, ALU.bitwise_and)
+        ts(X("la"), lists, 1536.0, AD)
+        cp(X("vz", 3, 2164, 144), X("ki"))
+        cp(X("ca"), IND(X("AO", C, PAD), X("la")))
+
+        def vgt(a, b):
+            tt(X("mn", 16 * a, 16 * b), IND(X("VY", 0, C), X("ca", a, b)), X("vcx", 16 * a, 16 * b), ALU.is_gt)
+        vgt(128, V2)
+        ts(X("cah"), X("ca"), -1536.0, AD)
+        embed()
+        mm(X("P1", 0, 128), X("am", p=(0, 1)), X("c524", p=(0, 1)), False, False)
+        for i, d0 in enumerate(range(V2, D, 32)):
+            act(X("gy", 512 * i, 512 * i + 512), IND(X("VY", 0, C), X("ca", d0, d0 + 32)))
+            mm(X("P%d" % (5 + i)), X("Ib"), X("gy", 512 * i, 512 * i + 512), False, True)
+        for i, d0 in enumerate(range(V2, D, 32)):
+            act(X("mn", 16 * d0, 16 * d0 + 512), X("P%d" % (5 + i)), AF.Sign)
+        vgt(0, 128)
+        reduce(128, V2, "blk")
+        for d0 in range(V2, D - 32, 32):
+            reduce(d0, d0 + 32, "hblk")
+        reduce(0, 128, "blk")
+        close(0)
+        reduce(D - 32, D, "hblk")
+        close(1)
+        if not last:
+            expand_z(t + 1)
+        best_of(0)
+        best_of(1)
+        ts(X("rn"), best, MAGIC, AD, MAGIC, SU)
+        ts(X("ver"), best, 12.0 * 65536 - 1536, ALU.is_ge)
+        tt(X("af"), best, X("rn"), SU)
+        tt(X("nz"), X("af"), X("hT"), ALU.not_equal)
+        tt(X("df"), X("af"), X("hT"), SU)
+        tt(X("prop"), X("nz"), X("ver"), ALU.is_gt)
+        cp(X("vz", 1, 2162, 144), X("af"))
+        mm(X("P2", 144, 152), X("U"), X("prop", 0, 8), True, True)
+        mm(X("P2", 152, 160), X("U"), X("prop", 8, 16), True, False)
+        mm(X("P2", 152, 160), X("on"), X("prop", 0, 8), False, True)
+        tt(X("rp"), X("P2", 144, 160), X("prop"), MU)
+        for i in range(16):
+            ts(X("oh", 64 * i, 64 * i + 64), X("io64"), X("rp", i, i + 1), EQ)
+            hf, gg = i // 8, i % 8
+            mm(X("P2", 0, 64), X("vz", 128 * gg + 1152 * hf, 128 * gg + 1152 * hf + 128), X("oh", 64 * i, 64 * i + 64), i == 0, i == 15)
+            if i == 0:
+                tt(X("df"), X("df"), X("ver"), MU)
+            if i == 11:
+                tt(X("hn"), X("df"), X("hT"), AD)
+        cp(X("rs16"), X("P2", 0, 64))
+        if not last:
+            conv_a(X("hn"))
+        for v, nm in enumerate(("sb0", "sb1", "sb2", "se3")):
+            mm(X("P3", 64 * v, 64 * v + 64), X(nm), X("rs16"), True, True)
+        for q in range(4):
+            o, w = blocks[q]
+            for hh in range(2):
+                mm(X("P4", o + hh * w, o + hh * w + w), X("Ib"), X("mk", 0, w), True, False)
+                mm(X("P4", o + hh * w, o + hh * w + w), X("sb%d" % hh), X("rs16", 16 * q, 64), False, True)
+        mm(X("P2", 64, 128), X("Ib"), X("k3072"), True, False)
+        tt(X("LM", 0, 192), X("P3", 0, 192), X("m256", 0, 192), MU)
+        ts(X("K64"), X("P3", 192, 256), X("kcode"), EQ)
+        scan(X("LS", 0, 192), X("rst", 0, 192), X("LM", 0, 192), AD)
+        cp(X("gl", 0, 12), X("LS", 15, 192, 16))
+        tt(X("prod"), IND(X("AO", 0, C), X("gl", 4, 8)), X("K64"), MU)
+        mm(X("P2", 64, 128), X("bo"), X("prod"), False, True)
+        if not last:
+            conv_b()
+            ts(X("hsend", 32 * t + 16, 32 * t + 32), X("hn"), 1536.0, AD)
+        mm(X("P7", 0, 64), X("Ib"), X("k8192"), True, False)
+        mm(X("P7", 0, 64), X("se4n"), X("rs16"), False, False)
+        ecol = [0]
+
+        def pairs(bank, q, ls, fin):
+            o, w = blocks[q]
+            e = ecol[0]
+            if e + 2 * w > 1280:
+                e = 0
+            ecol[0] = e + 2 * w
+            ts(X("E", e, e + 2 * w), X(bank, o, o + 2 * w), X("LS", ls, ls + 1), EQ)
+            for hh in range(2):
+                mm(X("P7", 16 * q, 64), X("boh"), X("E", e + hh * w, e + hh * w + w), False, fin and hh == 1)
+        for q in range(2):
+            for v in range(2):
+                pairs("P4", q, 64 * v + 16 * q + 15, False)
+        for q in range(4):
+            o, w = blocks[q]
+            mm(X("P5", o, o + w), X("Ib"), X("mk", 0, w), True, False)
+            mm(X("P5", o, o + w), X("sb2"), X("rs16", 16 * q, 64), False, True)
+        if not last:
+            ts(X("hsend", 32 * t, 32 * t + 16), lists, 1536.0, AD)
+            send(T.cores[(rank + HOP) % N], "hsend", 32 * t, 32 * t + 32, "hin", 32 * t, "ah%d" % (t + 1), "lh")
+        ts(X("rb16"), X("P2", 64, 128), -4608.0, AD)
+        tt(X("LM", 192, 256), X("P2", 64, 128), X("m256", 0, 64), MU)
+        for q in range(4):
+            o, w = blocks[q]
+            mm(X("P5", o + w, o + 2 * w), X("Ib"), X("mkb", 0, w), True, False)
+            mm(X("P5", o + w, o + 2 * w), X("se0"), X("rb16", 16 * q, 64), False, True)
+        scan(X("LS", 192, 256), X("rst", 0, 64), X("LM", 192, 256), AD)
+        cp(X("gl", 12, 16), X("LS", 207, 256, 16))
+        act(X("vg"), IND(X("VY", 0, PAD), X("gl")))
+        for q in range(2, 4):
+            for v in range(2):
+                pairs("P4", q, 64 * v + 16 * q + 15, False)
+        if not last:
+            mm(X("P6", 0, 64), X("se0"), X("rb16"), True, False)
+            mm(X("P6", 0, 64), X("se2n"), X("rs16"), False, True)
+            mm(X("P6", 64, 128), X("se0n"), X("rb16"), True, False)
+            mm(X("P6", 64, 128), X("se2"), X("rs16"), False, True)
+            mm(X("P6", 128, 192), X("sd"), X("rs16"), True, True)
+            mm(X("P6", 192, 256), X("sdn"), X("rs16"), True, True)
+        for q in (3, 2, 1, 0):
+            for v in range(2):
+                pairs("P5", q, 128 + 64 * v + 16 * q + 15, q == 0 and v == 1)
+        for o, ya, yb in ((0, "Inb", "Ib"), (64, "Ib", "Inb")):
+            mm(X("P3", 256 + o, 320 + o), X("Ib"), X("vg", o, o + 64), True, False)
+            mm(X("P3", 256 + o, 320 + o), X(ya), X("vg", 128, 192), False, False)
+            mm(X("P3", 256 + o, 320 + o), X(yb), X("vg", 192, 256), False, True)
+        act(X("nv"), X("P3", 256, 384))
+        mm(X("P2", 160, 288, 1, (0, 16)), X("hn"), X("If"), True, True)
+        act(X("hob", 128 * t, 128 * t + 128, 1, (0, 16)), X("P2", 160, 288, 1, (0, 16)), AF.Copy, 1536.0)
+        if not last:
+            for v in range(4):
+                tt(X("KD", 64 * v, 64 * v + 64), X("P6", 64 * v, 64 * v + 64), X("K64"), MU)
+            tt(X("NW"), IND(X("AO", 0, PAD), X("gl")), X("KD"), AD)
+        nq = 2 if last else 4
+        for v in range(nq):
+            tt(X("PM", 64 * v, 64 * v + 64), X("P7", 0, 64), X("DP", 64 * v, 64 * v + 64), ALU.min)
+        scan(X("PS", 0, 64 * nq), X("rst", 0, 64 * nq), X("PM", 0, 64 * nq), AD)
+        tt(X("of", 0, 4 * nq), X("PS", 15, 64 * nq, 16), X("LS", 15, 64 * nq, 16), ALU.max)
+        cp(X("so", 0, 4 * nq), X("of", 0, 4 * nq))
+        if not last:
+            cp(IND(X("AO"), X("so")), X("NW"))
+        cp(IND(X("VY"), X("so", 0, 8)), X("nv"))
+        for hf in range(2):
+            c0 = t * D + hf * 128
+            dma("S", (T.ho[:, c0:c0 + 128], []), X("hob", 128 * t, 128 * t + 128, 1, (8 * hf, 8 * hf + 8)))
+    dma("S", (T.vo[:, :], []), X("VY", 0, C))
+    for sem, v in sorted(cnt.items()):
+        if seen["G"].get(sem, 0) < v:
+            g.wait_ge(T.sem[sem], v)

@@ -4,26 +4,26 @@ from concourse.mybir import AluOpType as ALU, ActivationFunctionType as AF
 N, C, D, S, HOP = 4, 3072, 256, 4, 1
 PAD = 2 * C
 V1, V2 = 192, 160
+VOH = 11
 MAGIC = 1.5 * 2.0 ** 35
 F, B, H, I32, U16 = "float32", "bfloat16", "float16", "int32", "uint16"
 SCRATCH = {}
 for _n, _w, _d in (
         ("aoraw", C, I32), ("AO", PAD + 256, I32), ("VY", PAD + 256, B), ("z0", D, B), ("zin", 3 * D, B),
-        ("z16a", 16 * D, B), ("z16b", 16 * D, B), ("mn", 16 * D, B), ("gy", 1536, B), ("vc", D, B), ("vcx", 16 * V2, B),
+        ("z16a", 16 * D, B), ("z16b", 16 * D, B), ("mn", 16 * D, B), ("gy", 1536, B), ("vc", D, B), ("vcx", 16 * D, B),
         ("hdi", 16, I32), ("hdo", 16, F), ("hl0", 16, U16), ("hin", 96, U16), ("hsend", 96, U16),
         ("ca", D, U16), ("cah", D, H), ("sc", D, F), ("rn", 16, F), ("af", 16, F), ("bi", 16, I32), ("ki", 16, I32),
         ("TM", D, H), ("la", 16, U16), ("hT", 16, F), ("hn", 16, F), ("ver", 16, F), ("nz", 16, F), ("prop", 16, B), ("df", 16, F), ("rp", 16, F),
-        ("vz", 2304, H), ("oh", 1024, H), ("rs16", 64, H), ("rb16", 64, H), ("LM", D, F), ("LS", D, F), ("gl", 16, U16),
-        ("K64", 64, F), ("prod", 64, F), ("E", 1280, H), ("KD", D, F), ("NW", D, I32), ("vg", D, B), ("nv", 128, B),
+        ("vz", 2304, H), ("oh", 1024, B), ("sq", 1280, F), ("rs16", 64, H), ("rb16", 64, H), ("LM", D, F), ("LS", D, F), ("gl", 16, U16),
+        ("K64", 64, F), ("prod", 64, F), ("E", 1280, B), ("KD", D, F), ("NW", D, I32), ("vg", D, B), ("nv", 128, B),
         ("PM", D, F), ("PS", D, F), ("of", 16, F), ("so", 16, U16), ("hob", 512, F),
-        ("ipi", 1, I32), ("ip", 1, F), ("p16i", 1, I32), ("pgi", 1, I32), ("p16", 1, F), ("pg", 1, F), ("kcode", 1, F), ("sv", 16, F),
+        ("ipi", 1, I32), ("ip", 1, F), ("p16i", 1, I32), ("pgi", 1, I32), ("p16", 1, F), ("pg", 1, F), ("kcode", 1, F), ("sv", 16, F), ("ub", 1, F),
         ("i128", 128, F), ("imod", D, F), ("idiv", 128, F), ("ipad", D, F),
-        ("If", 128, F), ("Ih", 128, H), ("Ib", 128, B), ("Inb", 128, B), ("U", 128, B), ("on", 128, B), ("m256", D, F), ("bo", 128, F),
-        ("boh", 128, H), ("jjh", 8, H), ("blk", 8, B), ("nblk", 8, B), ("hblk", 8, B), ("zblk", 128, B), ("rst", D, F), ("brow", 128, B),
-        ("am", 128, B), ("c524", 128, B), ("io64", 64, H), ("exl", 16, U16), ("mk", 64, B), ("mkb", 64, B),
-        ("DP", D, F), ("k8192", 64, B), ("k3072", 64, B), ("hneg", 512, B),
-        ("se0", 128, H), ("se2", 128, H), ("se3", 128, H), ("se4n", 128, H), ("se0n", 128, H), ("se2n", 128, H),
-        ("sd", 128, H), ("sdn", 128, H), ("sb0", 128, H), ("sb1", 128, H), ("sb2", 128, H)):
+        ("If", 128, F), ("Ib", 128, B), ("Inb", 128, B), ("U", 128, B), ("on", 128, B), ("m256", D, F), ("bo", 128, F),
+        ("boh", 128, B), ("jj", 8, B), ("blk", 8, B), ("nblk", 8, B), ("zblk", 128, B), ("rst", D, F), ("brow", 128, B),
+        ("io64", 64, B), ("exl", 8, U16), ("mk", 64, B), ("mkb", 64, B), ("DP", D, F), ("k8192", 64, B), ("k3072", 64, B),
+        ("se0", 128, B), ("se2", 128, B), ("se3", 128, B), ("se4n", 128, B), ("se0n", 128, B), ("se2n", 128, B),
+        ("sd", 128, B), ("sdn", 128, B), ("sb0", 128, B), ("sb1", 128, B), ("sb2", 128, B)):
     SCRATCH[_n] = ("sbuf", [128, _w], _d)
 for _i in range(8):
     SCRATCH["P%d" % _i] = ("psum", [128, 512], F)
@@ -111,15 +111,15 @@ def rank_program(g, core, T, topo):
     def tt(o, a, b, f):
         op("V", lambda: g.vector.tensor_tensor(o[0], a[0], b[0], f), [o], [a, b])
 
+    def val(x, rs):
+        if isinstance(x, tuple):
+            rs.append(x)
+            return x[0]
+        return x
+
     def ts(o, a, s1, f1, s2=None, f2=None):
         rs = [a]
-        v1, v2 = s1, s2
-        if isinstance(s1, tuple):
-            rs.append(s1)
-            v1 = s1[0]
-        if isinstance(s2, tuple):
-            rs.append(s2)
-            v2 = s2[0]
+        v1, v2 = val(s1, rs), val(s2, rs)
         if f2 is None:
             op("V", lambda: g.vector.tensor_scalar(o[0], a[0], v1, None, f1), [o], rs)
         else:
@@ -128,8 +128,10 @@ def rank_program(g, core, T, topo):
     def scan(o, d0, d1, f1):
         op("V", lambda: g.vector.tensor_tensor_scan(o[0], d0[0], d1[0], 0.0, ALU.mult, f1), [o], [d0, d1])
 
-    def act(o, i, f=AF.Copy, bias=0.0):
-        op("A", lambda: g.scalar.activation(o[0], i[0], f, bias=bias), [o], [i])
+    def act(o, i, f=AF.Copy, bias=0.0, scale=1.0):
+        rs = [i]
+        b, c = val(bias, rs), val(scale, rs)
+        op("A", lambda: g.scalar.activation(o[0], i[0], f, bias=b, scale=c), [o], rs)
 
     def mm(o, l, r, start, stop):
         op("P", lambda: g.tensor.matmul(o[0], l[0], r[0], start, stop), [o], [l, r])
@@ -167,8 +169,8 @@ def rank_program(g, core, T, topo):
     EQ, MU, AD, SU = ALU.is_equal, ALU.mult, ALU.add, ALU.subtract
     dma("S", X("hdi"), (T.hd[:, :], []))
     dma("A", X("z0"), (T.zc[:, :], []))
+    w = C // 4
     for i in range(4):
-        w = C // 4
         dma("SA"[i % 2], X("aoraw", i * w, i * w + w), (T.ao[:, i * w:i * w + w], []))
     dma("S", X("VY", C, C + C // 2), (T.yd[:, 0:C // 2], []))
     dma("A", X("VY", C + C // 2, PAD), (T.yd[:, C // 2:C], []))
@@ -181,7 +183,7 @@ def rank_program(g, core, T, topo):
     iota(X("idiv"), [[1, 8], [0, 16]], 0, 0)
     iota(X("on"), [[0, 128]], 1, 0)
     iota(X("ipad"), [[1, 256]], PAD, 0)
-    iota(X("c524"), [[0, 128]], 524288, 0)
+    iota(X("io64"), [[1, 64]], 1, 0)
     iota(X("mk", 16, 64), [[0, 48]], 0, 0)
     iota(X("mkb", 16, 64), [[0, 48]], 4608, 0)
     iota(X("k8192"), [[0, 64]], 8192, 0)
@@ -193,92 +195,71 @@ def rank_program(g, core, T, topo):
     p, p16, pg = X("ip"), X("p16"), X("pg")
     ts(X("p16i"), X("ipi"), 15, ALU.bitwise_and)
     ts(X("pgi"), X("ipi"), 4, ALU.logical_shift_right)
-    op("V", lambda: g.vector.memset(T.hneg[:, :], -0.5), [X("hneg")], [])
-    cp(X("hl0"), X("hdi"))
-    ts(X("hdo"), X("hdi"), -1536.0, AD)
+    ts(X("If"), X("i128"), p, EQ)
     cp(X("p16"), X("p16i"))
     cp(X("pg"), X("pgi"))
-    cp(X("exl"), X("i128", 0, 16))
-    ts(X("jjh"), X("i128", 0, 8), pg, EQ)
+    ts(X("vz", 0, 256), X("imod"), 0.0, MU)
+    cp(X("vz", 256, 512), X("vz", 0, 256))
+    cp(X("vz", 512, 1024), X("vz", 0, 512))
+    cp(X("vz", 1024, 2048), X("vz", 0, 1024))
+    cp(X("vz", 2048, 2304), X("vz", 0, 256))
+    ts(X("vz", 4, 2165, 144), X("imod", 0, 16), 0.0, MU, 1.0, AD)
+    cp(X("hl0"), X("hdi"))
+    ts(X("hdo"), X("hdi"), -1536.0, AD)
+    ts(X("jj"), X("i128", 0, 8), pg, EQ)
+    ts(X("bo"), X("idiv"), pg, EQ)
+    cp(X("exl"), X("i128", 0, 8))
     ts(X("m256"), X("imod"), p16, EQ)
-    ts(X("Ib"), X("i128"), p, EQ)
-    ts(X("Inb"), X("i128"), p, EQ, -1.0, MU)
-    ts(X("Ih"), X("i128"), p, EQ)
-    ts(X("blk"), X("i128", 0, 8), pg, EQ, 65536.0, MU)
-    ts(X("nblk"), X("i128", 0, 8), pg, EQ, -65536.0, MU)
-    ts(X("hblk"), X("i128", 0, 8), pg, EQ, 32768.0, MU)
-    ts(X("zblk"), X("idiv"), pg, EQ, 65536.0, MU)
-    ts(X("brow"), X("imod", 0, 128), -4096.0, MU, 61440.0, AD)
-    ts(X("rst"), X("imod"), 0.0, ALU.not_equal)
-
-    def consts2():
-        ts(X("am"), X("i128"), float(V2 - 128), ALU.is_ge)
-        ts(X("U"), X("i128"), p, ALU.is_ge)
-        ts(X("If"), X("i128"), p, EQ)
-        ts(X("bo"), X("idiv"), pg, EQ)
-        ts(X("boh"), X("idiv"), pg, EQ, 8192.0, MU)
-        ts(X("kcode"), p16, -1.0, MU, 15.0, AD)
-        ts(X("io64"), X("i128", 0, 64), 1.0, AD)
-        for v in range(5):
-            ts(X("sv", v, v + 1), p16, float(v), EQ)
-        for v, c in ((0, 1536.0), (1, 1536.0), (2, 4608.0)):
-            ts(X("sv", 5 + v, 6 + v), p16, 4.0, EQ, c, MU)
-            tt(X("sv", 8 + v, 9 + v), X("sv", v, v + 1), X("sv", 5 + v, 6 + v), AD)
-
-    def consts3():
-        bo = X("bo")
-        for nm, v in (("se0", 0), ("se2", 2), ("se3", 3), ("sb0", 8), ("sb1", 9), ("sb2", 10)):
-            ts(X(nm), bo, X("sv", v, v + 1), MU)
-        ts(X("se4n"), bo, X("sv", 4, 5), MU, -8192.0, MU)
-        ts(X("se0n"), X("se0"), -1.0, MU)
-        ts(X("se2n"), X("se2"), -1.0, MU)
-        tt(X("sd"), X("sb1"), X("sb0"), SU)
-        ts(X("sdn"), X("sd"), -1.0, MU)
-
-    def consts4():
-        ts(X("mk", 0, 16), X("imod", 0, 16), p16, ALU.is_le, 16384.0, MU)
-        ts(X("mkb", 0, 16), X("mk", 0, 16), 4608.0, AD)
-        tt(X("DP"), X("m256"), X("ipad"), MU)
-        ts(X("vz", 0, 256), X("imod"), 0.0, MU)
-        cp(X("vz", 256, 512), X("vz", 0, 256))
-        cp(X("vz", 512, 1024), X("vz", 0, 512))
-        cp(X("vz", 1024, 2048), X("vz", 0, 1024))
-        cp(X("vz", 2048, 2304), X("vz", 0, 256))
-        ts(X("vz", 4, 2165, 144), X("imod", 0, 16), 0.0, MU, 1.0, AD)
+    sv = lambda i: X("sv", i, i + 1)
+    for v in range(4):
+        ts(sv(v), p16, float(v), EQ)
+    for i, c in ((4, -8192.0), (5, 1536.0), (6, 4608.0)):
+        ts(sv(i), p16, 4.0, EQ, c, MU)
+    tt(sv(8), sv(0), sv(5), AD)
+    tt(sv(9), sv(1), sv(5), AD)
+    tt(sv(10), sv(2), sv(6), AD)
+    tt(sv(11), sv(1), sv(0), SU)
+    ts(X("mk", 0, 16), X("imod", 0, 16), p16, ALU.is_le, 16384.0, MU)
+    act(X("Ib"), X("If"))
+    act(X("Inb"), X("If"), scale=-1.0)
+    act(X("brow"), X("imod", 0, 128), bias=61440.0, scale=-4096.0)
+    act(X("rst"), X("imod"), AF.Sign)
+    act(X("ub"), p, bias=100.0, scale=-200.0)
+    act(X("U"), X("i128"), AF.Sigmoid, X("ub"), 200.0)
+    for k in range(16):
+        act(X("z16a", k, 16 * D, 16), X("z0"))
+    act(X("blk"), X("jj"), scale=65536.0)
+    act(X("nblk"), X("jj"), scale=-65536.0)
+    bo = X("bo")
+    act(X("zblk"), bo, scale=65536.0)
+    act(X("boh"), bo, scale=8192.0)
+    act(X("kcode"), p16, bias=15.0, scale=-1.0)
+    act(X("mkb", 0, 16), X("mk", 0, 16), bias=4608.0)
+    for nm, v in (("se0", 0), ("se2", 2), ("se3", 3), ("se4n", 4), ("sb0", 8), ("sb1", 9), ("sb2", 10), ("sd", 11)):
+        act(X(nm), bo, scale=sv(v))
+    for nm, src in (("se0n", "se0"), ("se2n", "se2"), ("sdn", "sd")):
+        act(X(nm), X(src), scale=-1.0)
     blocks = []
     o = 0
     for q in range(4):
         blocks.append((o, 64 - 16 * q))
         o += 2 * (64 - 16 * q)
-
-    def expand_z(t):
-        src = X("z0") if t == 0 else X("zin", (t - 1) * D, t * D)
-        for k in range(16):
-            act(X(("z16a", "z16b")[t % 2], k, 16 * D, 16), src)
-
-    expand_z(0)
     for i in range(4):
-        w = C // 4
         ts(X("AO", i * w, i * w + w), X("aoraw", i * w, i * w + w), 4095, ALU.bitwise_and)
-        ts(X("AO", C + i * w, C + i * w + w), X("aoraw", i * w, i * w + w), 12, ALU.logical_shift_right)
-        (consts2, consts3, consts4, lambda: None)[i]()
 
-    def conv_a(src):
-        tt(X("TM"), IND(src, X("exl")), X("m256"), MU)
+    half = lambda nm, hf: X(nm, 8 * hf, 8 * hf + 8)
 
-    lists = X("P2", 128, 144)
+    def conv_a(nm, hf):
+        tt(X("TM", 128 * hf, 128 * hf + 128), IND(half(nm, hf), X("exl")), X("m256", 128 * hf, 128 * hf + 128), MU)
 
-    def conv_b():
-        for hf in range(2):
-            mm(X("P2", 128 + 8 * hf, 136 + 8 * hf), X("TM", 128 * hf, 128 * hf + 128), X("jjh"), True, True)
+    def conv_b(out, hf):
+        mm(out, X("TM", 128 * hf, 128 * hf + 128), X("jj"), True, True)
 
-    conv_a(X("hdo"))
-    conv_b()
-    cp(X("hT"), lists)
+    lists = lambda hf: X("P2" if hf == 0 else "P3", 384, 392)
 
     def embed():
         for hf in range(2):
-            mm(X("P%d" % hf, 0, 128), X("cah", 128 * hf, 128 * hf + 128), X("Ih"), True, False)
+            mm(X("P%d" % hf, 0, 128), X("cah", 128 * hf, 128 * hf + 128), X("Ib"), True, False)
 
     def reduce(d0, d1, w):
         hf, b = d0 // 128, d0 % 128
@@ -291,29 +272,30 @@ def rank_program(g, core, T, topo):
     def best_of(hf):
         scan(X("sc", 128 * hf, 128 * hf + 128), X("rst", 0, 128), X("P%d" % hf, 0, 128), ALU.max)
 
-    na1, na2 = (D - V1) // 32, (D - V2) // 32
     best = X("sc", 15, 256, 16)
+    bst = lambda hf: X("sc", 128 * hf + 15, 128 * hf + 128, 16)
     for t in range(S):
         last = t == S - 1
         hl = X("hl0") if t == 0 else X("hin", (t - 1) * 32, (t - 1) * 32 + 16)
         zrow = X("z0", V1, D) if t == 0 else X("zin", (t - 1) * D + V1, t * D)
         z16 = ("z16a", "z16b")[t % 2]
+        if not last:
+            for k in range(16):
+                zo, zi = X(("z16a", "z16b")[(t + 1) % 2], k, 16 * D, 16), X("zin", t * D, t * D + D)
+                op("G", lambda: g.affine_select(zo[0], zi[0], [[0, D]], ALU.is_ge, 0.0, 0, 0), [zo], [zi])
         for i, d0 in enumerate(range(V1, D, 32)):
             mm(X("P%d" % (3 + i)), X("Ib"), X(z16, 16 * d0, 16 * d0 + 512), True, False)
         cp(X("ca"), IND(X("AO", 0, C), hl))
         ts(X("cah"), X("ca"), -1536.0, AD)
         embed()
         mm(X("P1", 0, 128, 1, (64, 128)), zrow, X("zblk"), False, False)
-        for i in range(na2):
-            mm(X("P%d" % (5 + i)), X("Ib"), X("hneg"), True, False)
 
         def vmin(a, b):
             tt(X("mn", 16 * a, 16 * b), IND(X("VY", C, PAD), X("ca", a, b)), X(z16, 16 * a, 16 * b), ALU.min)
-
-        def sub_vc(i):
-            for j in range(16):
-                mm(X("P%d" % (5 + i), j, 512, 16), X("Inb"), X("vc", V2 + 32 * i, V2 + 32 * i + 32), False, False)
-        vmin(128, V1)
+        if t == 0:
+            for i in range(4):
+                ts(X("AO", C + i * w, C + i * w + w), X("aoraw", i * w, i * w + w), 12, ALU.logical_shift_right)
+        vmin(0, 128)
         for i, d0 in enumerate(range(V1, D, 32)):
             act(X("gy", 512 * i, 512 * i + 512), IND(X("VY", C, PAD), X("ca", d0, d0 + 32)))
             mm(X("P%d" % (3 + i)), X("Inb"), X("gy", 512 * i, 512 * i + 512), False, True)
@@ -321,57 +303,63 @@ def rank_program(g, core, T, topo):
             act(X("mn", 16 * d0, 16 * d0 + 512), X("P%d" % (3 + i)), AF.Relu)
         act(X("vc"), IND(X("VY", 0, C), hl))
         for j in range(16):
-            act(X("vcx", j, 16 * V2, 16), X("vc", 0, V2))
-        reduce(128, V1, "blk")
-        vmin(0, 64)
-        reduce(0, 64, "blk")
-        vmin(64, 96)
-        reduce(V1, D, "nblk")
-        close(1)
-        reduce(64, 96, "blk")
-        vmin(96, 128)
-        reduce(96, 128, "blk")
+            act(X("vcx", j, 16 * D, 16), X("vc"))
+        reduce(V1, V1 + 32, "nblk")
+        reduce(0, 128, "blk")
         close(0)
-        sub_vc(0)
-        if t:
+        vmin(128, 160)
+        reduce(128, 160, "blk")
+        vmin(160, V1)
+        reduce(V1 + 32, D, "nblk")
+        reduce(160, V1, "blk")
+        close(1)
+        if t == 0:
+            for hf in range(2):
+                conv_a("hdo", hf)
+                conv_b(lists(hf), hf)
+                cp(half("hT", hf), lists(hf))
+        else:
             ts(X("hT"), X("hin", (t - 1) * 32 + 16, t * 32), -1536.0, AD)
         cp(X("vz", 0, 2161, 144), X("hT"))
-        best_of(1)
         best_of(0)
-        ts(X("rn"), best, MAGIC, AD, MAGIC, SU)
-        tt(X("af"), best, X("rn"), SU)
-        conv_a(X("af"))
-        conv_b()
-        for i in range(1, na2):
-            sub_vc(i)
+        ts(half("rn", 0), bst(0), MAGIC, AD, MAGIC, SU)
+        tt(half("af", 0), bst(0), half("rn", 0), SU)
+        best_of(1)
+        conv_a("af", 0)
+        ts(half("rn", 1), bst(1), MAGIC, AD, MAGIC, SU)
+        conv_b(lists(0), 0)
+        cp(X("vz", 2, 1011, 144), half("af", 0))
+        tt(half("af", 1), bst(1), half("rn", 1), SU)
+        ts(half("la", 0), lists(0), 1536.0, AD)
+        conv_a("af", 1)
+        conv_b(lists(1), 1)
+        cp(X("ca", 0, 128), IND(X("AO", C, PAD), half("la", 0)))
+        ts(half("la", 1), lists(1), 1536.0, AD)
+        cp(X("vz", 1154, 2163, 144), half("af", 1))
+        cp(X("ca", 128, 256), IND(X("AO", C, PAD), half("la", 1)))
         ts(X("bi"), X("rn"), 1.0 / 4096, MU)
-        cp(X("vz", 2, 2163, 144), X("af"))
-        ts(X("ki"), X("bi"), 15, ALU.bitwise_and)
-        ts(X("la"), lists, 1536.0, AD)
-        cp(X("vz", 3, 2164, 144), X("ki"))
-        cp(X("ca"), IND(X("AO", C, PAD), X("la")))
+        for i, d0 in enumerate(range(V2, D, 32)):
+            mm(X("P%d" % (5 + i)), X("Inb"), X("vcx", 16 * d0, 16 * d0 + 512), True, False)
 
         def vgt(a, b):
             tt(X("mn", 16 * a, 16 * b), IND(X("VY", 0, C), X("ca", a, b)), X("vcx", 16 * a, 16 * b), ALU.is_gt)
-        vgt(128, V2)
         ts(X("cah"), X("ca"), -1536.0, AD)
-        embed()
-        mm(X("P1", 0, 128), X("am", p=(0, 1)), X("c524", p=(0, 1)), False, False)
+        vgt(0, 128)
         for i, d0 in enumerate(range(V2, D, 32)):
             act(X("gy", 512 * i, 512 * i + 512), IND(X("VY", 0, C), X("ca", d0, d0 + 32)))
             mm(X("P%d" % (5 + i)), X("Ib"), X("gy", 512 * i, 512 * i + 512), False, True)
         for i, d0 in enumerate(range(V2, D, 32)):
-            act(X("mn", 16 * d0, 16 * d0 + 512), X("P%d" % (5 + i)), AF.Sign)
-        vgt(0, 128)
-        reduce(128, V2, "blk")
-        for d0 in range(V2, D - 32, 32):
-            reduce(d0, d0 + 32, "hblk")
+            act(X("mn", 16 * d0, 16 * d0 + 512), X("P%d" % (5 + i)), AF.Sigmoid, -100.0, 200.0)
+        ts(X("ki"), X("bi"), 15, ALU.bitwise_and)
+        vgt(128, V2)
+        cp(X("vz", 3, 2164, 144), X("ki"))
+        embed()
         reduce(0, 128, "blk")
         close(0)
-        reduce(D - 32, D, "hblk")
+        reduce(128, 256, "blk")
         close(1)
-        if not last:
-            expand_z(t + 1)
+        if t == 0:
+            tt(X("DP"), X("m256"), X("ipad"), MU)
         best_of(0)
         best_of(1)
         ts(X("rn"), best, MAGIC, AD, MAGIC, SU)
@@ -385,79 +373,94 @@ def rank_program(g, core, T, topo):
         mm(X("P2", 152, 160), X("U"), X("prop", 8, 16), True, False)
         mm(X("P2", 152, 160), X("on"), X("prop", 0, 8), False, True)
         tt(X("rp"), X("P2", 144, 160), X("prop"), MU)
+        for i in range(VOH, 16):
+            act(X("sq", 64 * (i - VOH), 64 * (i - VOH) + 64), X("io64"), AF.Square, X("rp", i, i + 1), -1.0)
+        for i in range(VOH, 16):
+            act(X("oh", 64 * i, 64 * i + 64), X("sq", 64 * (i - VOH), 64 * (i - VOH) + 64), AF.Relu, 1.0, -1.0)
         for i in range(16):
-            ts(X("oh", 64 * i, 64 * i + 64), X("io64"), X("rp", i, i + 1), EQ)
+            if i < VOH:
+                ts(X("oh", 64 * i, 64 * i + 64), X("io64"), X("rp", i, i + 1), EQ)
             hf, gg = i // 8, i % 8
             mm(X("P2", 0, 64), X("vz", 128 * gg + 1152 * hf, 128 * gg + 1152 * hf + 128), X("oh", 64 * i, 64 * i + 64), i == 0, i == 15)
-            if i == 0:
-                tt(X("df"), X("df"), X("ver"), MU)
-            if i == 11:
-                tt(X("hn"), X("df"), X("hT"), AD)
+        tt(X("df"), X("df"), X("ver"), MU)
         cp(X("rs16"), X("P2", 0, 64))
-        if not last:
-            conv_a(X("hn"))
+        tt(X("hn"), X("df"), X("hT"), AD)
         for v, nm in enumerate(("sb0", "sb1", "sb2", "se3")):
             mm(X("P3", 64 * v, 64 * v + 64), X(nm), X("rs16"), True, True)
-        for q in range(4):
-            o, w = blocks[q]
-            for hh in range(2):
-                mm(X("P4", o + hh * w, o + hh * w + w), X("Ib"), X("mk", 0, w), True, False)
-                mm(X("P4", o + hh * w, o + hh * w + w), X("sb%d" % hh), X("rs16", 16 * q, 64), False, True)
         mm(X("P2", 64, 128), X("Ib"), X("k3072"), True, False)
+
+        def rows(bank, q, hh, nm, src, m):
+            o, wd = blocks[q]
+            mm(X(bank, o + hh * wd, o + hh * wd + wd), X("Ib"), X(m, 0, wd), True, False)
+            mm(X(bank, o + hh * wd, o + hh * wd + wd), X(nm), X(src, 16 * q, 64), False, True)
+        for q in range(4):
+            rows("P4", q, 0, "sb0", "rs16", "mk")
+            rows("P4", q, 1, "sb1", "rs16", "mk")
         tt(X("LM", 0, 192), X("P3", 0, 192), X("m256", 0, 192), MU)
         ts(X("K64"), X("P3", 192, 256), X("kcode"), EQ)
         scan(X("LS", 0, 192), X("rst", 0, 192), X("LM", 0, 192), AD)
         cp(X("gl", 0, 12), X("LS", 15, 192, 16))
         tt(X("prod"), IND(X("AO", 0, C), X("gl", 4, 8)), X("K64"), MU)
-        mm(X("P2", 64, 128), X("bo"), X("prod"), False, True)
-        if not last:
-            conv_b()
-            ts(X("hsend", 32 * t + 16, 32 * t + 32), X("hn"), 1536.0, AD)
-        mm(X("P7", 0, 64), X("Ib"), X("k8192"), True, False)
-        mm(X("P7", 0, 64), X("se4n"), X("rs16"), False, False)
-        ecol = [0]
-
-        def pairs(bank, q, ls, fin):
-            o, w = blocks[q]
-            e = ecol[0]
-            if e + 2 * w > 1280:
-                e = 0
-            ecol[0] = e + 2 * w
-            ts(X("E", e, e + 2 * w), X(bank, o, o + 2 * w), X("LS", ls, ls + 1), EQ)
-            for hh in range(2):
-                mm(X("P7", 16 * q, 64), X("boh"), X("E", e + hh * w, e + hh * w + w), False, fin and hh == 1)
-        for q in range(2):
-            for v in range(2):
-                pairs("P4", q, 64 * v + 16 * q + 15, False)
+        mm(X("P2", 64, 128), bo, X("prod"), False, True)
         for q in range(4):
-            o, w = blocks[q]
-            mm(X("P5", o, o + w), X("Ib"), X("mk", 0, w), True, False)
-            mm(X("P5", o, o + w), X("sb2"), X("rs16", 16 * q, 64), False, True)
+            rows("P5", q, 0, "sb2", "rs16", "mk")
         if not last:
-            ts(X("hsend", 32 * t, 32 * t + 16), lists, 1536.0, AD)
-            send(T.cores[(rank + HOP) % N], "hsend", 32 * t, 32 * t + 32, "hin", 32 * t, "ah%d" % (t + 1), "lh")
+            conv_a("hn", 0)
+            conv_a("hn", 1)
+            ts(X("hsend", 32 * t + 16, 32 * t + 32), X("hn"), 1536.0, AD)
         ts(X("rb16"), X("P2", 64, 128), -4608.0, AD)
         tt(X("LM", 192, 256), X("P2", 64, 128), X("m256", 0, 64), MU)
-        for q in range(4):
-            o, w = blocks[q]
-            mm(X("P5", o + w, o + 2 * w), X("Ib"), X("mkb", 0, w), True, False)
-            mm(X("P5", o + w, o + 2 * w), X("se0"), X("rb16", 16 * q, 64), False, True)
         scan(X("LS", 192, 256), X("rst", 0, 64), X("LM", 192, 256), AD)
         cp(X("gl", 12, 16), X("LS", 207, 256, 16))
-        act(X("vg"), IND(X("VY", 0, PAD), X("gl")))
-        for q in range(2, 4):
-            for v in range(2):
-                pairs("P4", q, 64 * v + 16 * q + 15, False)
+        for q in range(4):
+            rows("P5", q, 1, "se0", "rb16", "mkb")
         if not last:
+            for hf in range(2):
+                conv_b(X("P2", 128 + 8 * hf, 136 + 8 * hf), hf)
+            ts(X("hsend", 32 * t, 32 * t + 16), X("P2", 128, 144), 1536.0, AD)
+            send(T.cores[(rank + HOP) % N], "hsend", 32 * t, 32 * t + 32, "hin", 32 * t, "ah%d" % (t + 1), "lh")
             mm(X("P6", 0, 64), X("se0"), X("rb16"), True, False)
             mm(X("P6", 0, 64), X("se2n"), X("rs16"), False, True)
             mm(X("P6", 64, 128), X("se0n"), X("rb16"), True, False)
             mm(X("P6", 64, 128), X("se2"), X("rs16"), False, True)
             mm(X("P6", 128, 192), X("sd"), X("rs16"), True, True)
             mm(X("P6", 192, 256), X("sdn"), X("rs16"), True, True)
-        for q in (3, 2, 1, 0):
+        mm(X("P7", 0, 64), X("Ib"), X("k8192"), True, False)
+        mm(X("P7", 0, 64), X("se4n"), X("rs16"), False, False)
+        pr = {}
+        e = 0
+        for bank, base in (("P4", 0), ("P5", 128)):
+            for q in range(4):
+                o, wd = blocks[q]
+                for v in range(2):
+                    ls = base + 64 * v + 16 * q + 15
+                    pr[bank, q, v] = (X(bank, o, o + 2 * wd), X("LS", ls, ls + 1), e, wd)
+                    e += 2 * wd
+
+        def count(key, fin=False):
+            _, _, e, wd = pr[key]
+            for hh in range(2):
+                mm(X("P7", 64 - wd, 64), X("boh"), X("E", e + hh * wd, e + hh * wd + wd), False, fin and hh == 1)
+
+        def by_scalar(keys):
+            for key in keys:
+                src, col, e, wd = pr[key]
+                act(X("sq", e, e + 2 * wd), src, AF.Square, col, -1.0)
+            for key in keys:
+                src, col, e, wd = pr[key]
+                act(X("E", e, e + 2 * wd), X("sq", e, e + 2 * wd), AF.Relu, 1.0, -1.0)
+                count(key)
+
+        def by_vector(key):
+            src, col, e, wd = pr[key]
+            ts(X("E", e, e + 2 * wd), src, col, EQ)
+        by_scalar([("P4", q, v) for q in range(4) for v in range(2)])
+        by_scalar([("P5", q, v) for q in (2, 3) for v in range(2)])
+        act(X("vg"), IND(X("VY", 0, PAD), X("gl")))
+        for q in (1, 0):
             for v in range(2):
-                pairs("P5", q, 128 + 64 * v + 16 * q + 15, q == 0 and v == 1)
+                by_vector(("P5", q, v))
+                count(("P5", q, v), q == 0 and v == 1)
         for o, ya, yb in ((0, "Inb", "Ib"), (64, "Ib", "Inb")):
             mm(X("P3", 256 + o, 320 + o), X("Ib"), X("vg", o, o + 64), True, False)
             mm(X("P3", 256 + o, 320 + o), X(ya), X("vg", 128, 192), False, False)

import numpy as np
from concourse.mybir import AluOpType as ALU, ActivationFunctionType as AF

N, C, D, S, HOP = 4, 3072, 256, 4, 1
PAD = 2 * C
V1, V2 = 192, 160
VOH = 11
MAGIC = 1.5 * 2.0 ** 35
F, B, H, I32, U16 = "float32", "bfloat16", "float16", "int32", "uint16"
SCRATCH = {}
for _n, _w, _d in (
        ("aoraw", C, I32), ("AO", PAD + 256, I32), ("VY", PAD + 256, B), ("z0", D, B), ("zin", 3 * D, B),
        ("z16a", 16 * D, B), ("z16b", 16 * D, B), ("mn", 16 * D, B), ("gy", 1536, B), ("vc", D, B), ("vcx", 16 * D, B),
        ("hdi", 16, I32), ("hdo", 16, F), ("hl0", 16, U16), ("hin", 96, U16), ("hsend", 96, U16),
        ("ca", D, U16), ("cah", D, H), ("sc", D, F), ("rn", 16, F), ("af", 16, F), ("bi", 16, I32), ("ki", 16, I32),
        ("TM", D, H), ("la", 16, U16), ("hT", 16, F), ("hn", 16, F), ("ver", 16, F), ("nz", 16, F), ("prop", 16, B), ("df", 16, F), ("rp", 16, F),
        ("vz", 2304, H), ("oh", 1024, B), ("sq", 1280, F), ("rs16", 64, H), ("rb16", 64, H), ("LM", D, F), ("LS", D, F), ("gl", 16, U16),
        ("K64", 64, F), ("prod", 64, F), ("E", 1280, B), ("KD", D, F), ("NW", D, I32), ("vg", D, B), ("nv", 128, B),
        ("PM", D, F), ("PS", D, F), ("of", 16, F), ("so", 16, U16), ("hob", 512, F),
        ("ipi", 1, I32), ("ip", 1, F), ("p16i", 1, I32), ("pgi", 1, I32), ("p16", 1, F), ("pg", 1, F), ("kcode", 1, F), ("sv", 16, F), ("ub", 1, F),
        ("i128", 128, F), ("imod", D, F), ("idiv", 128, F), ("ipad", D, F),
        ("If", 128, F), ("Ib", 128, B), ("Inb", 128, B), ("U", 128, B), ("on", 128, B), ("m256", D, F), ("bo", 128, F),
        ("boh", 128, B), ("jj", 8, B), ("blk", 8, B), ("nblk", 8, B), ("zblk", 128, B), ("rst", D, F), ("brow", 128, B),
        ("io64", 64, B), ("exl", 8, U16), ("mk", 64, B), ("mkb", 64, B), ("DP", D, F), ("k8192", 64, B), ("k3072", 64, B),
        ("se0", 128, B), ("se2", 128, B), ("se3", 128, B), ("se4n", 128, B), ("se0n", 128, B), ("se2n", 128, B),
        ("sd", 128, B), ("sdn", 128, B), ("sb0", 128, B), ("sb1", 128, B), ("sb2", 128, B)):
    SCRATCH[_n] = ("sbuf", [128, _w], _d)
for _i in range(8):
    SCRATCH["P%d" % _i] = ("psum", [128, 512], F)
SEMAPHORES = ["cV", "cA", "cP", "cG"] + ["d%d" % i for i in range(24)] + ["az1", "az2", "az3", "ah1", "ah2", "ah3", "lz", "lh"]


def rank_program(g, core, T, topo):
    rank = T.rank_of(core)
    if rank is None:
        return
    Q = {"V": g.vector, "A": g.scalar, "P": g.tensor, "G": g, "S": g.sync}
    cnt = {}
    seen = {q: {} for q in Q}
    snap = {}
    Wr, Rd = {}, {}
    toks = [None]

    def new_token(q, sem, n):
        cnt[sem] = cnt.get(sem, 0) + n
        toks.append((sem, cnt[sem], q))
        snap[len(toks) - 1] = dict(seen[q])
        return len(toks) - 1

    def wait_tok(q, i):
        sem, v, _ = toks[i]
        if seen[q].get(sem, 0) >= v:
            return
        Q[q].wait_ge(T.sem[sem], v)
        seen[q][sem] = v
        for s2, v2 in snap[i].items():
            if v2 > seen[q].get(s2, 0):
                seen[q][s2] = v2

    def track(name):
        if name not in Wr:
            Wr[name] = np.zeros(SCRATCH[name][1][1], np.int64)
            Rd[name] = {}

    def need(q, reads, writes):
        ids = set()
        for kind, accs in ((0, reads), (1, writes)):
            for name, cols in accs:
                track(name)
                if SCRATCH[name][0] == "psum":
                    for arr in list(Rd[name].values()) + [Wr[name]]:
                        ids.update(int(x) for x in np.unique(arr) if x and toks[int(x)][2] != q)
                else:
                    ids.update(int(x) for x in np.unique(Wr[name][cols]))
                    if kind:
                        for arr in Rd[name].values():
                            ids.update(int(x) for x in np.unique(arr[cols]))
        ids.discard(0)
        if q == "P":
            ids = {i for i in ids if toks[i][0] != "cP"}
        for i in sorted(ids, reverse=True):
            wait_tok(q, i)

    def note(tok, reads, writes):
        key = toks[tok][0]
        for name, cols in reads:
            Rd[name].setdefault(key, np.zeros(len(Wr[name]), np.int64))[cols] = tok
        for name, cols in writes:
            Wr[name][cols] = tok

    def op(q, call, writes, reads):
        rr = [a for x in reads for a in x[1]]
        ww = [a for x in writes for a in x[1]]
        need(q, rr, ww)
        call().then_inc(T.sem["c" + q], 1)
        note(new_token(q, "c" + q, 1), rr, ww)

    def X(name, a=None, b=None, s=1, p=None):
        a = 0 if a is None else a
        b = SCRATCH[name][1][1] if b is None else b
        ps = slice(None) if p is None else slice(p[0], p[1])
        ap = T[name][ps, a:b] if s == 1 else T[name][ps, a:b:s]
        return (ap, [(name, np.arange(a, b, s))])

    def IND(win, off):
        return (win[0].indirect(off[0]), win[1] + off[1])

    def cp(o, i):
        op("V", lambda: g.vector.tensor_copy(o[0], i[0]), [o], [i])

    def tt(o, a, b, f):
        op("V", lambda: g.vector.tensor_tensor(o[0], a[0], b[0], f), [o], [a, b])

    def val(x, rs):
        if isinstance(x, tuple):
            rs.append(x)
            return x[0]
        return x

    def ts(o, a, s1, f1, s2=None, f2=None):
        rs = [a]
        v1, v2 = val(s1, rs), val(s2, rs)
        if f2 is None:
            op("V", lambda: g.vector.tensor_scalar(o[0], a[0], v1, None, f1), [o], rs)
        else:
            op("V", lambda: g.vector.tensor_scalar(o[0], a[0], v1, v2, f1, f2), [o], rs)

    def scan(o, d0, d1, f1):
        op("V", lambda: g.vector.tensor_tensor_scan(o[0], d0[0], d1[0], 0.0, ALU.mult, f1), [o], [d0, d1])

    def act(o, i, f=AF.Copy, bias=0.0, scale=1.0):
        rs = [i]
        b, c = val(bias, rs), val(scale, rs)
        op("A", lambda: g.scalar.activation(o[0], i[0], f, bias=b, scale=c), [o], rs)

    def mm(o, l, r, start, stop):
        op("P", lambda: g.tensor.matmul(o[0], l[0], r[0], start, stop), [o], [l, r])

    def iota(o, pat, base, cm):
        if SCRATCH[o[1][0][0]][2] == I32:
            op("G", lambda: g.iota(o[0], pat, base, cm), [o], [])
        else:
            op("G", lambda: g.iota(o[0], pat, base, cm, allow_small_or_imprecise_dtypes=True), [o], [])

    nd = [0]

    def dma(q, o, i):
        need(q, i[1], o[1])
        sem = "d%d" % nd[0]
        nd[0] += 1
        Q[q].dma_start(o[0], i[0]).then_inc(T.sem[sem], 16)
        note(new_token(q, sem, 16), i[1], o[1])

    def send(dst, name, a, b, name2, a2, rsem, lsem):
        src = X(name, a, b)
        need("G", src[1], [])
        rid, pid, _ = topo.addr(dst)
        eng = topo.engines(core, dst)[:8]
        g.remote_dma(T[name2][:, a2:a2 + b - a], src[0], T.sem[rsem], T.sem[lsem], pid, rid, sum(1 << e for e in eng))
        note(new_token("G", lsem, len(eng)), src[1], [])

    def arrives(name, a, b, rsem, src):
        track(name)
        cnt[rsem] = len(topo.engines(src, core)[:8])
        toks.append((rsem, cnt[rsem], "R"))
        snap[len(toks) - 1] = {}
        Wr[name][a:b] = len(toks) - 1

    EQ, MU, AD, SU = ALU.is_equal, ALU.mult, ALU.add, ALU.subtract
    dma("S", X("hdi"), (T.hd[:, :], []))
    dma("A", X("z0"), (T.zc[:, :], []))
    w = C // 4
    for i in range(4):
        dma("SA"[i % 2], X("aoraw", i * w, i * w + w), (T.ao[:, i * w:i * w + w], []))
    dma("S", X("VY", C, C + C // 2), (T.yd[:, 0:C // 2], []))
    dma("A", X("VY", C + C // 2, PAD), (T.yd[:, C // 2:C], []))
    dma("S", X("VY", 0, C // 2), (T.ve[:, 0:C // 2], []))
    dma("A", X("VY", C // 2, C), (T.ve[:, C // 2:C], []))
    iota(X("ipi"), [[0, 1]], 0, 1)
    iota(X("ip"), [[0, 1]], 0, 1)
    iota(X("i128"), [[1, 128]], 0, 0)
    iota(X("imod"), [[0, 16], [1, 16]], 0, 0)
    iota(X("idiv"), [[1, 8], [0, 16]], 0, 0)
    iota(X("on"), [[0, 128]], 1, 0)
    iota(X("ipad"), [[1, 256]], PAD, 0)
    iota(X("io64"), [[1, 64]], 1, 0)
    iota(X("mk", 16, 64), [[0, 48]], 0, 0)
    iota(X("mkb", 16, 64), [[0, 48]], 4608, 0)
    iota(X("k8192"), [[0, 64]], 8192, 0)
    iota(X("k3072"), [[0, 64]], 3072, 0)
    for r in range(1, N):
        send(T.cores[(rank + r * HOP) % N], "z0", 0, D, "zin", (r - 1) * D, "az%d" % r, "lz")
        arrives("zin", (r - 1) * D, r * D, "az%d" % r, T.cores[(rank - r * HOP) % N])
        arrives("hin", (r - 1) * 32, r * 32, "ah%d" % r, T.cores[(rank - HOP) % N])
    p, p16, pg = X("ip"), X("p16"), X("pg")
    ts(X("p16i"), X("ipi"), 15, ALU.bitwise_and)
    ts(X("pgi"), X("ipi"), 4, ALU.logical_shift_right)
    ts(X("If"), X("i128"), p, EQ)
    cp(X("p16"), X("p16i"))
    cp(X("pg"), X("pgi"))
    ts(X("vz", 0, 256), X("imod"), 0.0, MU)
    cp(X("vz", 256, 512), X("vz", 0, 256))
    cp(X("vz", 512, 1024), X("vz", 0, 512))
    cp(X("vz", 1024, 2048), X("vz", 0, 1024))
    cp(X("vz", 2048, 2304), X("vz", 0, 256))
    ts(X("vz", 4, 2165, 144), X("imod", 0, 16), 0.0, MU, 1.0, AD)
    cp(X("hl0"), X("hdi"))
    ts(X("hdo"), X("hdi"), -1536.0, AD)
    ts(X("jj"), X("i128", 0, 8), pg, EQ)
    ts(X("bo"), X("idiv"), pg, EQ)
    cp(X("exl"), X("i128", 0, 8))
    ts(X("m256"), X("imod"), p16, EQ)
    sv = lambda i: X("sv", i, i + 1)
    for v in range(4):
        ts(sv(v), p16, float(v), EQ)
    for i, c in ((4, -8192.0), (5, 1536.0), (6, 4608.0)):
        ts(sv(i), p16, 4.0, EQ, c, MU)
    tt(sv(8), sv(0), sv(5), AD)
    tt(sv(9), sv(1), sv(5), AD)
    tt(sv(10), sv(2), sv(6), AD)
    tt(sv(11), sv(1), sv(0), SU)
    ts(X("mk", 0, 16), X("imod", 0, 16), p16, ALU.is_le, 16384.0, MU)
    act(X("Ib"), X("If"))
    act(X("Inb"), X("If"), scale=-1.0)
    act(X("brow"), X("imod", 0, 128), bias=61440.0, scale=-4096.0)
    act(X("rst"), X("imod"), AF.Sign)
    act(X("ub"), p, bias=100.0, scale=-200.0)
    act(X("U"), X("i128"), AF.Sigmoid, X("ub"), 200.0)
    for k in range(16):
        act(X("z16a", k, 16 * D, 16), X("z0"))
    act(X("blk"), X("jj"), scale=65536.0)
    act(X("nblk"), X("jj"), scale=-65536.0)
    bo = X("bo")
    act(X("zblk"), bo, scale=65536.0)
    act(X("boh"), bo, scale=8192.0)
    act(X("kcode"), p16, bias=15.0, scale=-1.0)
    act(X("mkb", 0, 16), X("mk", 0, 16), bias=4608.0)
    for nm, v in (("se0", 0), ("se2", 2), ("se3", 3), ("se4n", 4), ("sb0", 8), ("sb1", 9), ("sb2", 10), ("sd", 11)):
        act(X(nm), bo, scale=sv(v))
    for nm, src in (("se0n", "se0"), ("se2n", "se2"), ("sdn", "sd")):
        act(X(nm), X(src), scale=-1.0)
    blocks = []
    o = 0
    for q in range(4):
        blocks.append((o, 64 - 16 * q))
        o += 2 * (64 - 16 * q)
    for i in range(4):
        ts(X("AO", i * w, i * w + w), X("aoraw", i * w, i * w + w), 4095, ALU.bitwise_and)

    half = lambda nm, hf: X(nm, 8 * hf, 8 * hf + 8)

    def conv_a(nm, hf):
        tt(X("TM", 128 * hf, 128 * hf + 128), IND(half(nm, hf), X("exl")), X("m256", 128 * hf, 128 * hf + 128), MU)

    def conv_b(out, hf):
        mm(out, X("TM", 128 * hf, 128 * hf + 128), X("jj"), True, True)

    lists = lambda hf: X("P2" if hf == 0 else "P3", 384, 392)

    def embed():
        for hf in range(2):
            mm(X("P%d" % hf, 0, 128), X("cah", 128 * hf, 128 * hf + 128), X("Ib"), True, False)

    def reduce(d0, d1, w):
        hf, b = d0 // 128, d0 % 128
        for k in range(16):
            mm(X("P%d" % hf, k, 128, 16, (b, b + d1 - d0)), X("mn", 16 * d0 + k, 16 * d1, 16), X(w), False, False)

    def close(hf):
        mm(X("P%d" % hf, 0, 128), X("on", p=(0, 1)), X("brow", p=(0, 1)), False, True)

    def best_of(hf):
        scan(X("sc", 128 * hf, 128 * hf + 128), X("rst", 0, 128), X("P%d" % hf, 0, 128), ALU.max)

    best = X("sc", 15, 256, 16)
    bst = lambda hf: X("sc", 128 * hf + 15, 128 * hf + 128, 16)
    for t in range(S):
        last = t == S - 1
        hl = X("hl0") if t == 0 else X("hin", (t - 1) * 32, (t - 1) * 32 + 16)
        zrow = X("z0", V1, D) if t == 0 else X("zin", (t - 1) * D + V1, t * D)
        z16 = ("z16a", "z16b")[t % 2]
        if not last:
            for k in range(16):
                zo, zi = X(("z16a", "z16b")[(t + 1) % 2], k, 16 * D, 16), X("zin", t * D, t * D + D)
                op("G", lambda: g.affine_select(zo[0], zi[0], [[0, D]], ALU.is_ge, 0.0, 0, 0), [zo], [zi])
        for i, d0 in enumerate(range(V1, D, 32)):
            mm(X("P%d" % (3 + i)), X("Ib"), X(z16, 16 * d0, 16 * d0 + 512), True, False)
        cp(X("ca"), IND(X("AO", 0, C), hl))
        ts(X("cah"), X("ca"), -1536.0, AD)
        embed()
        mm(X("P1", 0, 128, 1, (64, 128)), zrow, X("zblk"), False, False)

        def vmin(a, b):
            tt(X("mn", 16 * a, 16 * b), IND(X("VY", C, PAD), X("ca", a, b)), X(z16, 16 * a, 16 * b), ALU.min)
        if t == 0:
            for i in range(4):
                ts(X("AO", C + i * w, C + i * w + w), X("aoraw", i * w, i * w + w), 12, ALU.logical_shift_right)
        vmin(0, 128)
        for i, d0 in enumerate(range(V1, D, 32)):
            act(X("gy", 512 * i, 512 * i + 512), IND(X("VY", C, PAD), X("ca", d0, d0 + 32)))
            mm(X("P%d" % (3 + i)), X("Inb"), X("gy", 512 * i, 512 * i + 512), False, True)
        for i, d0 in enumerate(range(V1, D, 32)):
            act(X("mn", 16 * d0, 16 * d0 + 512), X("P%d" % (3 + i)), AF.Relu)
        act(X("vc"), IND(X("VY", 0, C), hl))
        for j in range(16):
            act(X("vcx", j, 16 * D, 16), X("vc"))
        reduce(V1, V1 + 32, "nblk")
        reduce(0, 128, "blk")
        close(0)
        vmin(128, 160)
        reduce(128, 160, "blk")
        vmin(160, V1)
        reduce(V1 + 32, D, "nblk")
        reduce(160, V1, "blk")
        close(1)
        if t == 0:
            for hf in range(2):
                conv_a("hdo", hf)
                conv_b(lists(hf), hf)
                cp(half("hT", hf), lists(hf))
        else:
            ts(X("hT"), X("hin", (t - 1) * 32 + 16, t * 32), -1536.0, AD)
        cp(X("vz", 0, 2161, 144), X("hT"))
        best_of(0)
        ts(half("rn", 0), bst(0), MAGIC, AD, MAGIC, SU)
        tt(half("af", 0), bst(0), half("rn", 0), SU)
        best_of(1)
        conv_a("af", 0)
        ts(half("rn", 1), bst(1), MAGIC, AD, MAGIC, SU)
        conv_b(lists(0), 0)
        cp(X("vz", 2, 1011, 144), half("af", 0))
        tt(half("af", 1), bst(1), half("rn", 1), SU)
        ts(half("la", 0), lists(0), 1536.0, AD)
        conv_a("af", 1)
        conv_b(lists(1), 1)
        cp(X("ca", 0, 128), IND(X("AO", C, PAD), half("la", 0)))
        ts(half("la", 1), lists(1), 1536.0, AD)
        cp(X("vz", 1154, 2163, 144), half("af", 1))
        cp(X("ca", 128, 256), IND(X("AO", C, PAD), half("la", 1)))
        ts(X("bi"), X("rn"), 1.0 / 4096, MU)
        for i, d0 in enumerate(range(V2, D, 32)):
            mm(X("P%d" % (5 + i)), X("Inb"), X("vcx", 16 * d0, 16 * d0 + 512), True, False)

        def vgt(a, b):
            tt(X("mn", 16 * a, 16 * b), IND(X("VY", 0, C), X("ca", a, b)), X("vcx", 16 * a, 16 * b), ALU.is_gt)
        ts(X("cah"), X("ca"), -1536.0, AD)
        vgt(0, 128)
        for i, d0 in enumerate(range(V2, D, 32)):
            act(X("gy", 512 * i, 512 * i + 512), IND(X("VY", 0, C), X("ca", d0, d0 + 32)))
            mm(X("P%d" % (5 + i)), X("Ib"), X("gy", 512 * i, 512 * i + 512), False, True)
        for i, d0 in enumerate(range(V2, D, 32)):
            act(X("mn", 16 * d0, 16 * d0 + 512), X("P%d" % (5 + i)), AF.Sigmoid, -100.0, 200.0)
        ts(X("ki"), X("bi"), 15, ALU.bitwise_and)
        vgt(128, V2)
        cp(X("vz", 3, 2164, 144), X("ki"))
        embed()
        reduce(0, 128, "blk")
        close(0)
        reduce(128, 256, "blk")
        close(1)
        if t == 0:
            tt(X("DP"), X("m256"), X("ipad"), MU)
        best_of(0)
        best_of(1)
        ts(X("rn"), best, MAGIC, AD, MAGIC, SU)
        ts(X("ver"), best, 12.0 * 65536 - 1536, ALU.is_ge)
        tt(X("af"), best, X("rn"), SU)
        tt(X("nz"), X("af"), X("hT"), ALU.not_equal)
        tt(X("df"), X("af"), X("hT"), SU)
        tt(X("prop"), X("nz"), X("ver"), ALU.is_gt)
        cp(X("vz", 1, 2162, 144), X("af"))
        mm(X("P2", 144, 152), X("U"), X("prop", 0, 8), True, True)
        mm(X("P2", 152, 160), X("U"), X("prop", 8, 16), True, False)
        mm(X("P2", 152, 160), X("on"), X("prop", 0, 8), False, True)
        tt(X("rp"), X("P2", 144, 160), X("prop"), MU)
        for i in range(VOH, 16):
            act(X("sq", 64 * (i - VOH), 64 * (i - VOH) + 64), X("io64"), AF.Square, X("rp", i, i + 1), -1.0)
        for i in range(VOH, 16):
            act(X("oh", 64 * i, 64 * i + 64), X("sq", 64 * (i - VOH), 64 * (i - VOH) + 64), AF.Relu, 1.0, -1.0)
        for i in range(16):
            if i < VOH:
                ts(X("oh", 64 * i, 64 * i + 64), X("io64"), X("rp", i, i + 1), EQ)
            hf, gg = i // 8, i % 8
            mm(X("P2", 0, 64), X("vz", 128 * gg + 1152 * hf, 128 * gg + 1152 * hf + 128), X("oh", 64 * i, 64 * i + 64), i == 0, i == 15)
        tt(X("df"), X("df"), X("ver"), MU)
        cp(X("rs16"), X("P2", 0, 64))
        tt(X("hn"), X("df"), X("hT"), AD)
        for v, nm in enumerate(("sb0", "sb1", "sb2", "se3")):
            mm(X("P3", 64 * v, 64 * v + 64), X(nm), X("rs16"), True, True)
        mm(X("P2", 64, 128), X("Ib"), X("k3072"), True, False)

        def rows(bank, q, hh, nm, src, m):
            o, wd = blocks[q]
            mm(X(bank, o + hh * wd, o + hh * wd + wd), X("Ib"), X(m, 0, wd), True, False)
            mm(X(bank, o + hh * wd, o + hh * wd + wd), X(nm), X(src, 16 * q, 64), False, True)
        for q in range(4):
            rows("P4", q, 0, "sb0", "rs16", "mk")
            rows("P4", q, 1, "sb1", "rs16", "mk")
        tt(X("LM", 0, 192), X("P3", 0, 192), X("m256", 0, 192), MU)
        ts(X("K64"), X("P3", 192, 256), X("kcode"), EQ)
        scan(X("LS", 0, 192), X("rst", 0, 192), X("LM", 0, 192), AD)
        cp(X("gl", 0, 12), X("LS", 15, 192, 16))
        tt(X("prod"), IND(X("AO", 0, C), X("gl", 4, 8)), X("K64"), MU)
        mm(X("P2", 64, 128), bo, X("prod"), False, True)
        for q in range(4):
            rows("P5", q, 0, "sb2", "rs16", "mk")
        if not last:
            conv_a("hn", 0)
            conv_a("hn", 1)
            ts(X("hsend", 32 * t + 16, 32 * t + 32), X("hn"), 1536.0, AD)
        ts(X("rb16"), X("P2", 64, 128), -4608.0, AD)
        tt(X("LM", 192, 256), X("P2", 64, 128), X("m256", 0, 64), MU)
        scan(X("LS", 192, 256), X("rst", 0, 64), X("LM", 192, 256), AD)
        cp(X("gl", 12, 16), X("LS", 207, 256, 16))
        for q in range(4):
            rows("P5", q, 1, "se0", "rb16", "mkb")
        if not last:
            for hf in range(2):
                conv_b(X("P2", 128 + 8 * hf, 136 + 8 * hf), hf)
            ts(X("hsend", 32 * t, 32 * t + 16), X("P2", 128, 144), 1536.0, AD)
            send(T.cores[(rank + HOP) % N], "hsend", 32 * t, 32 * t + 32, "hin", 32 * t, "ah%d" % (t + 1), "lh")
            mm(X("P6", 0, 64), X("se0"), X("rb16"), True, False)
            mm(X("P6", 0, 64), X("se2n"), X("rs16"), False, True)
            mm(X("P6", 64, 128), X("se0n"), X("rb16"), True, False)
            mm(X("P6", 64, 128), X("se2"), X("rs16"), False, True)
            mm(X("P6", 128, 192), X("sd"), X("rs16"), True, True)
            mm(X("P6", 192, 256), X("sdn"), X("rs16"), True, True)
        mm(X("P7", 0, 64), X("Ib"), X("k8192"), True, False)
        mm(X("P7", 0, 64), X("se4n"), X("rs16"), False, False)
        pr = {}
        e = 0
        for bank, base in (("P4", 0), ("P5", 128)):
            for q in range(4):
                o, wd = blocks[q]
                for v in range(2):
                    ls = base + 64 * v + 16 * q + 15
                    pr[bank, q, v] = (X(bank, o, o + 2 * wd), X("LS", ls, ls + 1), e, wd)
                    e += 2 * wd

        def count(key, fin=False):
            _, _, e, wd = pr[key]
            for hh in range(2):
                mm(X("P7", 64 - wd, 64), X("boh"), X("E", e + hh * wd, e + hh * wd + wd), False, fin and hh == 1)

        def by_scalar(keys):
            for key in keys:
                src, col, e, wd = pr[key]
                act(X("sq", e, e + 2 * wd), src, AF.Square, col, -1.0)
            for key in keys:
                src, col, e, wd = pr[key]
                act(X("E", e, e + 2 * wd), X("sq", e, e + 2 * wd), AF.Relu, 1.0, -1.0)
                count(key)

        def by_vector(key):
            src, col, e, wd = pr[key]
            ts(X("E", e, e + 2 * wd), src, col, EQ)
        by_scalar([("P4", q, v) for q in range(4) for v in range(2)])
        by_scalar([("P5", q, v) for q in (2, 3) for v in range(2)])
        act(X("vg"), IND(X("VY", 0, PAD), X("gl")))
        for q in (1, 0):
            for v in range(2):
                by_vector(("P5", q, v))
                count(("P5", q, v), q == 0 and v == 1)
        for o, ya, yb in ((0, "Inb", "Ib"), (64, "Ib", "Inb")):
            mm(X("P3", 256 + o, 320 + o), X("Ib"), X("vg", o, o + 64), True, False)
            mm(X("P3", 256 + o, 320 + o), X(ya), X("vg", 128, 192), False, False)
            mm(X("P3", 256 + o, 320 + o), X(yb), X("vg", 192, 256), False, True)
        act(X("nv"), X("P3", 256, 384))
        mm(X("P2", 160, 288, 1, (0, 16)), X("hn"), X("If"), True, True)
        act(X("hob", 128 * t, 128 * t + 128, 1, (0, 16)), X("P2", 160, 288, 1, (0, 16)), AF.Copy, 1536.0)
        if not last:
            for v in range(4):
                tt(X("KD", 64 * v, 64 * v + 64), X("P6", 64 * v, 64 * v + 64), X("K64"), MU)
            tt(X("NW"), IND(X("AO", 0, PAD), X("gl")), X("KD"), AD)
        nq = 2 if last else 4
        for v in range(nq):
            tt(X("PM", 64 * v, 64 * v + 64), X("P7", 0, 64), X("DP", 64 * v, 64 * v + 64), ALU.min)
        scan(X("PS", 0, 64 * nq), X("rst", 0, 64 * nq), X("PM", 0, 64 * nq), AD)
        tt(X("of", 0, 4 * nq), X("PS", 15, 64 * nq, 16), X("LS", 15, 64 * nq, 16), ALU.max)
        cp(X("so", 0, 4 * nq), X("of", 0, 4 * nq))
        if not last:
            cp(IND(X("AO"), X("so")), X("NW"))
        cp(IND(X("VY"), X("so", 0, 8)), X("nv"))
        for hf in range(2):
            c0 = t * D + hf * 128
            dma("S", (T.ho[:, c0:c0 + 128], []), X("hob", 128 * t, 128 * t + 128, 1, (8 * hf, 8 * hf + 8)))
    dma("S", (T.vo[:, :], []), X("VY", 0, C))
    for sem, v in sorted(cnt.items()):
        if seen["G"].get(sem, 0) < v:
            g.wait_ge(T.sem[sem], v)
